import numpy as np, ml_dtypes
CORES = [23,119,17,113]
N = 4
BF = ml_dtypes.bfloat16
W, M, H, L, CAP, RO = 1024, 4096, 4096, 256, 40, 4
def sums(w, x):
    return np.add.reduce(w[..., 0:1] * x, axis=2) & 4095, np.add.reduce(w[..., 1:2] * x, axis=2) & 4095
def probe(w, lm, tl, mo, m):
    u, v = sums(w, m); a = (u * v) >> 5
    c = (a[:, :, None] + w[..., 2:3] * u[:, :, None]) & (W - 1)
    x = np.take_along_axis(lm, c.reshape(N, 8, 1, 16 * L), 3).reshape(N, 8, 16, 16, L)
    ok = np.all(x <= m[:, :, :, None], axis=2); has = np.any(ok, axis=2)
    g = np.take_along_axis(c, np.argmax(ok, axis=2)[:, :, None], 2)
    tg = np.take_along_axis(tl, g, 3); q = m - np.take_along_axis(lm, g, 3)
    y = np.take_along_axis(mo, tg.reshape(N, 8, 1, 16 * L), 3).reshape(N, 8, 16, 16, L)
    p = np.minimum(q[:, :, :, None] + y, 255).reshape(N, 8, 16, 16 * L)
    e, f = sums(w, p); h = (((e * f) >> 5) + e) & (H - 1)
    return a, c[:, :, 0], has, tg, p, h
def seek(sn, has, p, h):
    new = np.any(np.take_along_axis(sn, h[:, :, None], 3) != p, axis=2).reshape(N, 8, 16, L) & has[:, :, None]
    return np.any(new, axis=2), np.argmax(new, axis=2)
def first(key):
    o = np.argsort(key, axis=2, kind="stable"); s = np.take_along_axis(key, o, 2)
    b = np.ones(key.shape, bool); b[..., 1:] = s[..., 1:] != s[..., :-1]
    win = np.zeros(key.shape, bool); np.put_along_axis(win, o, b, 2); return win
def turn(st, pr, fill):
    lm, tl, sn, m, ct, ci = st; a, c0, has, tg, p, h = pr
    child, i = seek(sn, has, p, h); j = i * L + np.arange(L)
    pc = np.take_along_axis(p, j[:, :, None], 3); hc = np.take_along_axis(h, j, 2)
    win = first(np.where(child, hc, np.where(has, 2 ** 15 + np.arange(L), 2 ** 14 + c0)))
    wt = np.where(np.arange(16)[:, None] == ci[:, :, None], (a & (M - 1))[:, :, None], ct)
    lm, tl, sn = lm.copy(), tl.copy(), sn.copy()
    for r in range(N):
        for g in range(8):
            b = win[r, g] & child[r, g]; sn[r, g][:, hc[r, g, b]] = pc[r, g][:, b]
            b = win[r, g] & ~has[r, g]; lm[r, g][:, c0[r, g, b]] = m[r, g][:, b]; tl[r, g][:, c0[r, g, b]] = wt[r, g][:, b]
    nm, nt, ni = fill.copy(), tl[..., :L].copy(), np.zeros((N, 8, L), np.int64)
    for d in range(N):
        f = child & ((hc & (N - 1)) == d); f = f & (np.add.accumulate(f.astype(np.int64), axis=2) <= CAP)
        for r in range(N):
            for g in range(8):
                b = np.flatnonzero(f[r, g]); z = r * CAP + np.arange(b.size)
                nm[d, g][:, z] = pc[r, g][:, b]; nt[d, g][:, z] = tg[r, g][:, b]; ni[d, g, z] = i[r, g, b]
    return lm, tl, sn, nm, nt, ni
def mono(rng, n, den, top):
    return ((rng.random((N, 8, 16, n), dtype=np.float32) < den) * rng.integers(1, top + 1, (N, 8, 16, n), dtype=np.int32)).astype(np.int32)
def uneven(rng, n, den):
    v = np.exp2(8 * rng.random((N, 8, 1, n), dtype=np.float32) * rng.random((N, 8, 16, n), dtype=np.float32))
    return ((rng.random((N, 8, 16, n), dtype=np.float32) < den) * np.minimum(v, 255).astype(np.int32)).astype(np.int32)
def base(rng):
    w = np.tile(rng.integers(0, 128, (1, 8, 16, 3), dtype=np.int32), (N, 1, 1, 1)); dens = np.array([0.15, 0.5, 0.8, 1.0, 1.0])
    lm = mono(rng, W, rng.choice(np.array([0.2, 0.3, 0.5]), (N, 8, 1, W)), 160); mo = mono(rng, M, rng.choice(np.array([0.2, 0.4]), (N, 8, 1, M)), 120)
    tl = rng.integers(0, M, (N, 8, 16, W), dtype=np.int32)
    sn = np.where(rng.random((N, 8, 1, H)) < 0.5, -1, mono(rng, H, 0.5, 255)).astype(np.int32)
    m = mono(rng, L, rng.choice(dens, (N, 8, 1, L)), 255); fr = mono(rng, RO * L, rng.choice(dens, (N, 8, 1, RO * L)), 255)
    old = np.take_along_axis(m, rng.integers(0, L, (N, 8, 1, RO * L)), 3)
    return w, lm, tl, mo, sn, m, np.where(rng.random((N, 8, 1, RO * L)) < 0.3, old, fr)
def plant(rng, w, lm, tl, mo, sn, m, fr, until=1, n=L - N * CAP - 8):
    pr = probe(w, lm, tl, mo, m); a, c0, has, tg, p, h = pr; used = np.zeros((N, 8, H), bool)
    cnt = rng.choice(np.array([0, 1, 2, 5, 15, 16]), (N, 8, L), p=[0.5, 0.2, 0.15, 0.05, 0.05, 0.05])
    for r in range(N):
        for g in range(8):
            for k in (1, 2, 5, 15, 16):
                x = np.flatnonzero(has[r, g] & (cnt[r, g] == k)); j = (np.arange(k)[:, None] * L + x).reshape(-1)
                sn[r, g][:, h[r, g, j]] = p[r, g][:, j]; used[r, g, h[r, g, j]] = True
    st = (lm, tl, sn, m, tl[..., :L], np.zeros((N, 8, L), np.int64))
    for t in range(until):
        was, row = st[1], st[5]; st = turn(st, pr, fr[..., t * L:(t + 1) * L])
        pr = probe(w, st[0], st[1], mo, st[3])
    own = pr[0] & (M - 1); came = np.any(st[3] != fr[..., (until - 1) * L:until * L], axis=2)
    stale = ~pr[2] & ~came & (row > 0)
    lone = ~pr[2] & came; anew = ~pr[2] & ~came & ~stale & np.any(st[1][..., :L] != was[..., :L], axis=2)
    used = used | np.any(st[2] != sn, axis=2)
    for r in range(N):
        for g in range(8):
            x = np.flatnonzero(lone[r, g]); v = np.flatnonzero(anew[r, g])[:4]
            s0 = np.flatnonzero(stale[r, g])[:4]
            if x.size + v.size + s0.size == 0: continue
            o = np.concatenate([s0, v, np.resize(x, n - v.size - s0.size)]) if x.size else np.concatenate([s0, v])
            fr[r, g][:, until * L + N * CAP:until * L + N * CAP + o.size] = st[3][r, g][:, o]
            half = rng.random(x.size) < 0.5
            col = np.concatenate([st[4][r, g][:, x][np.arange(16)[:, None] < st[5][r, g, x]],
                own[r, g, x[half]], own[r, g, v]])
            for part, cs in ((True, own[r, g, x[~half]]), (False, col)):
                y = mo[r, g][:, cs]
                e = np.add.reduce(w[r, g, :, 0:1] * y, axis=0) & 4095; f = np.add.reduce(w[r, g, :, 1:2] * y, axis=0) & 4095
                z = (((e * f) >> 5) + e) & (H - 1); b = ~used[r, g, z]
                if part: y = np.where((y == 0) & (rng.random(y.shape) < rng.choice(np.array([0.1, 0.5]), (1, y.shape[1]))), -1, y)
                sn[r, g][:, z[b]] = y[:, b]
def pack(w, lm, tl, mo, sn, m, fr):
    d = {"lm": lm, "tl": tl, "mo": mo, "sn": sn, "fm": m, "fr": fr, "wk": w}
    return {k: np.ascontiguousarray(x.reshape(N, 128, -1)).astype(np.int32) if k in ("tl", "wk") else np.ascontiguousarray(x.reshape(N, 128, -1)).astype(np.float32).astype(BF) for k, x in d.items()}
def setup_inputs(rng):
    s = base(rng); plant(rng, *s); return pack(*s)
def setup_inputs_again(rng):
    w, lm, tl, mo, sn, m, fr = base(rng); w[:, 2, :, 2] = 0; w[:, 3, :, 0] = 0; lm[:, 0] = 255; lm[:, 1] = 0; lm[N - 1, 3, :, 0] = 0; sn[:] = -1
    few = np.tile(rng.integers(0, M, (1, 8, 1, 5), dtype=np.int32), (N, 1, 1, 1))
    tl = np.take_along_axis(few, rng.integers(0, 5, (N, 8, 16, W)), 3); tl[:, :, 7] = rng.integers(0, M, (N, 8, W))
    fr = np.take_along_axis(m, rng.integers(0, 12, (N, 8, 1, RO * L)), 3); m = np.take_along_axis(m, rng.integers(0, 12, (N, 8, 1, L)), 3)
    return pack(w, lm, tl, mo, sn, m, fr)
def setup_inputs_corners(rng):
    w, lm, tl, mo, sn, m, fr = base(rng)
    lm[:, :, 0] = np.where(np.any(lm > 0, axis=2), lm[:, :, 0], 1); tl[:, 5] = rng.choice(np.array([0, M - 1]), (N, 16, W))
    fr[..., ::7] = 0; fr[..., 3::7] = 255
    pool, to = [], []
    for z in range(2):
        x = mono(rng, L, 0.9, 255); pr = probe(w, lm, tl, mo, x); child, i = seek(sn, pr[2], pr[4], pr[5])
        hc = np.take_along_axis(pr[5], i * L + np.arange(L), 2); pool.append(x); to.append(np.where(child, hc & (N - 1), -1))
    pool = np.concatenate(pool, axis=3); to = np.concatenate(to, axis=2)
    for r in range(N):
        for g in range(8):
            left = L; lanes = []
            for e in range(N):
                n = int(rng.choice(np.array([0, 1, CAP - 1, CAP, CAP + 1, 2 * CAP])))
                if r == 0 and e == 0: n = (CAP, CAP + 1, CAP - 1, 0, 1, CAP, CAP + 1, 2 * CAP)[g]
                if r == N - 1 and e == 0: n = CAP
                x = np.flatnonzero(to[r, g] == (r + 1 + e) % N)[:min(n, left)]; lanes.append(x); left -= x.size
            x = np.concatenate(lanes); m[r, g] = 0; m[r, g][:, rng.permutation(L)[:x.size]] = pool[r, g][:, x]
    return pack(w, lm, tl, mo, sn, m, fr)
def setup_inputs_ends(rng):
    def sub(n, den):
        return 255 * (rng.random((N, 8, 16, n)) < den).astype(np.int32)
    w = 127 * rng.integers(0, 2, (8, 16, 3)); w[6, :, 0:2] = 127; w[7, :, 0:2] = 0; w[:, 0, 2] = 0; w[:, 15, 2] = 127
    w[7, 0:4, 0] = 127; w[7, 4:8, 1] = 127; w[7, 13:16, 0] = (127, 127, 3); w[7, 10:13, 1] = (127, 127, 3)
    w = np.tile(w[None], (N, 1, 1, 1)).astype(np.int32); dens = np.array([0.0, 0.3, 0.6, 0.9, 1.0])
    lm = sub(W, 0.15); mo = sub(M, 0.3); tl = (M - 1) * rng.integers(0, 2, (N, 8, 16, W))
    t = rng.integers(0, 3, (N, 8, 1, H)); sn = np.where(t == 0, -1, np.where(t == 1, 255, 256 * rng.integers(0, 2, (N, 8, 16, H)) - 1))
    m = sub(L, rng.choice(dens, (N, 8, 1, L))); fr = sub(RO * L, rng.choice(dens, (N, 8, 1, RO * L)))
    for x in (m, fr):
        x[..., 0] = 255; x[..., -1] = 255
        z = rng.random(x.shape[-1]) < 0.3; z[0] = True; z[-1] = True
        x[:, 7, 0:8][:, :, z] = 0; x[:, 7, 10:16][:, :, z] = 255
    return pack(w, lm, tl, mo, sn, m, fr)
def setup_inputs_late(rng):
    w, lm, tl, mo, sn, m, fr = base(rng)
    lm = mono(rng, W, rng.choice(np.array([0.5, 0.6]), (N, 8, 1, W)), 160)
    pool = mono(rng, 8192, 0.5, 255); u, v = sums(w, pool)
    aim = np.where(np.arange(8) % 2 == 1, H - 1, 0)[:, None]
    k = np.argmax(((((u * v) >> 5) + u) & (H - 1)) == aim, axis=2)
    mo[..., M - 1:] = np.take_along_axis(pool, k[:, :, None, None], 3); sn[..., 0] = -1; sn[..., H - 1] = -1
    x = mono(rng, 4, 0.6, 255); u, v = sums(w, x); c0 = (((u * v) >> 5) + w[:, :, 0, 2:3] * u) & (W - 1)
    np.put_along_axis(lm, c0[:, :, None], x, 3); np.put_along_axis(tl[:, :, 0], c0, M - 1, 2)
    for t in (1, 2):
        fr[..., t * L + N * CAP + 24:t * L + N * CAP + 28] = x
    one = mono(rng, 1, 0.4, 255)
    for g in (3, 4):
        fr[:, g, :, :L] = one[:, g]
    s = (w, lm, tl, mo, sn, m, fr); plant(rng, *s, until=2, n=24); return pack(*s)
def setup_inputs_spread(rng):
    w = np.tile((np.exp2(7 * rng.random((1, 8, 16, 3))) - 1).astype(np.int32), (N, 1, 1, 1)); dens = np.array([0.3, 0.7, 1.0])
    lm = uneven(rng, W, rng.choice(np.array([0.2, 0.4]), (N, 8, 1, W))); mo = uneven(rng, M, 0.4)
    tl = np.minimum(M * rng.random((N, 8, 16, W)) ** 3, M - 1).astype(np.int32); sn = uneven(rng, H, 0.7) - 1
    m = uneven(rng, L, rng.choice(dens, (N, 8, 1, L))); fr = uneven(rng, RO * L, rng.choice(dens, (N, 8, 1, RO * L)))
    s = (w, lm, tl, mo, sn, m, fr); plant(rng, *s); return pack(*s)
def check_inputs(d):
    bad = []
    for k, lo, hi in (("lm", 0, 255), ("tl", 0, M - 1), ("mo", 0, 255), ("sn", -1, 255), ("fm", 0, 255), ("fr", 0, 255), ("wk", 0, 127)):
        x = np.asarray(d[k]).astype(np.float32)
        if not (np.all(x >= lo) and np.all(x <= hi)): bad.append("range of " + k)
        elif np.any(x != np.floor(x)): bad.append("whole numbers in " + k)
    if np.any(d["wk"] != d["wk"][:1]): bad.append("wk alike on all ranks")
    return bad
def reference(lm, tl, mo, sn, fm, fr, wk):
    lead, tail, mon, seen, front, fill, w = [x.astype(np.float32).astype(np.int32).reshape(N, 8, 16, -1) for x in (lm, tl, mo, sn, fm, fr, wk)]
    st = (lead, tail, seen, front, tail[..., :L], np.zeros((N, 8, L), np.int64))
    for t in range(RO):
        st = turn(st, probe(w, st[0], st[1], mon, st[3]), fill[..., t * L:(t + 1) * L])
    return {"yl": st[0].reshape(N, 128, W).astype(np.float32).astype(BF), "yf": st[3].reshape(N, 128, L).astype(np.float32).astype(BF)}

@@ -1,0 +1,552 @@
+import numpy as np
+from concourse.bass import DstId, RemoteDMATransfer
+from concourse.mybir import AluOpType as O, ActivationFunctionType as F
+
+B, I32, F32, U16 = "bfloat16", "int32", "float32", "uint16"
+SHAPES = {
+    "wks": ([3], I32), "tli": ([1024], I32), "frs": ([1024], B), "LM": ([1296], B), "TL": ([1296], F32), "MO": ([4096], B),
+    "SN": ([6400], B), "ones": ([128], B), "BG": ([128], B), "ID": ([128], B), "TSs": ([128], B), "TS": ([128], B),
+    "nI": ([128], B), "IDf": ([128], F32), "nIf": ([128], F32), "BGf": ([128], F32), "TSf": ([128], F32), "LU": ([16, 128], B),
+    "LV": ([16, 128], B), "EX": ([16, 128], B), "WU": ([128], B), "WV": ([128], B), "wkf": ([3], F32), "nwk": ([3], F32),
+    "pi": ([8], I32), "pm": ([8], I32), "pmf": ([8], F32), "nm": ([256], F32), "nd": ([256], F32), "MD": ([256], F32),
+    "kr": ([256], B), "kpat": ([256], F32), "jt": ([256], B), "zi": ([64], F32), "zc": ([64], F32), "rt": ([4, 16], B),
+    "sd": ([2, 16], F32), "c255": ([64], B), "cbig": ([64], B), "itab": ([4096], B), "mp0": ([256], B), "mp1": ([256], B),
+    "uvi": ([32], I32), "uvm": ([32], I32), "kt": ([256], F32), "cc": ([256], I32), "cm": ([256], I32), "co": ([256], U16),
+    "V": ([4096], B), "ga": ([512], B), "gb": ([512], B), "ka": ([256], F32), "kc": ([256], F32), "ql": ([256], B),
+    "tg": ([256], U16), "t4": ([256], F32), "ya": ([256], F32), "ct": ([256], F32), "eq": ([256], F32), "wd": ([256], F32),
+    "wt": ([256], F32), "tla": ([160], I32), "cia": ([160], I32), "tmi": ([160], F32), "Y": ([4096], B), "P": ([4096], B),
+    "hi": ([256], I32), "hm": ([256], I32), "hs": ([128], I32), "ha": ([128], I32), "hb": ([128], I32), "hc": ([256], I32),
+    "h16": ([256], U16), "zk": ([256], F32), "M": ([4096], B), "kb": ([256], F32), "kd": ([256], F32), "D4": ([4, 16], B),
+    "t1": ([256], F32), "pc": ([256], F32), "o1": ([2, 16], F32), "o2": ([2, 16], F32), "kw": ([256], U16), "kdf": ([256], F32),
+    "E": ([16, 256], B), "dub": ([256], B), "xi": ([160], I32), "pa": ([160], I32), "inv": ([160], B), "ri": ([160], B),
+    "se": ([1280], F32), "rx": ([640], F32),
+}
+SUB = {"sni": ("M", 0, 4096), "lmi": ("Y", 0, 1024), "fmi": ("ga", 0, 256), "bg0": ("gb", 0, 128)}
+for name, typ, names in (
+        ("F16", F32, "nfb nk0 nk1 nk key los kl oL oS o3 lane dl ds ln8 ci16 ct16 cn16 uvf Awf kz"),
+        ("N16", I32, "uvs Aw k1 gi k3 n0 n1 rr hk nt"), ("H16", U16, "g16 n16 s16 oL16 oS16 repa repb")):
+    names = names.split()
+    SHAPES[name] = ([16 * len(names)], typ)
+    SUB.update({k: (name, 16 * i, 16) for i, k in enumerate(names)})
+PS = {"PX0": [1024], "PX1": [1024], "PU0": [512], "PU1": [512], "PK": [512], "PM": [32, 16]}
+SCRATCH = {k: ("sbuf", [128] + s, d) for k, (s, d) in SHAPES.items()}
+SCRATCH.update({k: ("psum", [128] + s, F32) for k, s in PS.items()})
+LOADS = ["wk", "fm", "lm", "tl", "mo", "sn", "fr"]
+SEMAPHORES = ["sv", "sa", "sp", "sg", "st", "ol", "of"] + ["ld" + k for k in LOADS] + ["ar%d" % t for t in range(4)]
+BIG = 131072.0
+TOP = 2097152
+NACT = 6
+SPLIT = (64, 64, 32, 32)
+
+
+def rank_program(g, core, T, topo):
+    rank = T.rank_of(core)
+    if rank is None:
+        return
+    eng = {"v": g.vector, "a": g.scalar, "p": g.tensor, "g": g, "s": g.sync}
+    sem = {"v": "sv", "a": "sa", "p": "sp", "g": "sg"}
+    IDX, lastw, lastr, bank = {}, {}, {}, {}
+    for k, s in list(PS.items()) + [(k, s) for k, (s, d) in SHAPES.items()]:
+        n = int(np.prod(s))
+        IDX[k] = np.arange(n).reshape(s)
+        lastw[k] = np.full(n, -1)
+        lastr[k] = {}
+    ops = []
+    count, clock = {}, {q: {} for q in eng}
+
+    def S(a, b, st=None):
+        return slice(a, b, st)
+    ALL = S(None, None)
+
+    def v(name, *idx):
+        if name in SUB:
+            name, o, n = SUB[name]
+            a, b, st = idx[0].indices(n)
+            idx = (S(o + a, o + b, st),)
+        return {"n": name, "ap": T[name][(ALL,) + idx], "c": IDX[name][idx].ravel(), "off": None}
+
+    def ind(win, off):
+        return {"n": win["n"], "ap": win["ap"].indirect(off["ap"]), "c": win["c"], "off": off}
+
+    def hazards(q, w, r):
+        need = set()
+        for x in list(r) + list(w):
+            if not (q == "p" and x["n"] in PS):
+                need.update(np.unique(lastw[x["n"]][x["c"]]).tolist())
+        for x in w:
+            for q2, a in lastr[x["n"]].items():
+                need.add(int(a[x["c"]].max()))
+        for x in list(w) + list(r):
+            if x["n"] in PS:
+                for b in np.unique(x["c"] // 512).tolist():
+                    need.update(o for q2, o in bank.get((x["n"], b), {}).items() if q2 != q)
+        need.discard(-1)
+        return need
+
+    def wait(q, need):
+        ck, best = clock[q], {}
+        for o in need:
+            q2, n, c2 = ops[o]
+            if ck.get(q2, 0) < n and (q2 not in best or ops[best[q2]][1] < n):
+                best[q2] = o
+        for q2 in sorted(best, key=lambda z: -best[z]):
+            q2, n, c2 = ops[best[q2]]
+            if ck.get(q2, 0) >= n:
+                continue
+            eng[q].wait_ge(T.sem[sem.get(q2, q2)], n)
+            for k, x in c2.items():
+                ck[k] = max(ck.get(k, 0), x)
+            ck[q2] = n
+
+    def note(q, tag, inc, w, r):
+        count[tag] = count.get(tag, 0) + inc
+        ops.append((tag, count[tag], dict(clock[q]) if q else {}))
+        o = len(ops) - 1
+        for x in w:
+            lastw[x["n"]][x["c"]] = o
+        for x in r:
+            lastr[x["n"]].setdefault(tag, np.full(lastw[x["n"]].size, -1))[x["c"]] = o
+        for x in list(w) + list(r):
+            if x["n"] in PS:
+                for b in np.unique(x["c"] // 512).tolist():
+                    bank.setdefault((x["n"], b), {})[tag] = o
+        return o
+
+    def do(q, fn, w, r):
+        r = r + [x["off"] for x in w + r if x["off"] is not None]
+        wait(q, hazards(q, w, r))
+        fn().then_inc(T.sem[sem[q]], 1)
+        note(q, q, 1, w, r)
+
+    def dma(q, tag, out, in_):
+        w, r = ([out] if "n" in out else []), ([in_] if "n" in in_ else [])
+        wait(q, hazards(q, w, r))
+        eng[q].dma_start(out["ap"], in_["ap"]).then_inc(T.sem[tag], 16)
+        return note(q, tag, 16, w, r)
+
+    def col(s):
+        return [s] if isinstance(s, dict) else []
+
+    def num(s):
+        return s["ap"] if isinstance(s, dict) else s
+
+    def ts(out, a, s1, op0, s2=None, op1=None):
+        if op1 is None:
+            do("v", lambda: g.vector.tensor_scalar(out["ap"], a["ap"], num(s1), None, op0), [out], [a] + col(s1))
+        else:
+            do("v", lambda: g.vector.tensor_scalar(out["ap"], a["ap"], num(s1), num(s2), op0, op1), [out], [a] + col(s1) + col(s2))
+
+    def tt(out, a, b, op):
+        do("v", lambda: g.vector.tensor_tensor(out["ap"], a["ap"], b["ap"], op), [out], [a, b])
+
+    def cp(out, a):
+        do("v", lambda: g.vector.tensor_copy(out["ap"], a["ap"]), [out], [a])
+
+    def fill(out, x):
+        do("v", lambda: g.vector.memset(out["ap"], x), [out], [])
+
+    def act(out, a, f=F.Identity, bias=0.0, scale=1.0):
+        do("a", lambda: g.scalar.activation(out["ap"], a["ap"], f, bias=num(bias), scale=num(scale)), [out], [a] + col(bias) + col(scale))
+
+    def mm(out, l, r, start, stop):
+        do("p", lambda: g.tensor.matmul(out["ap"], l["ap"], r["ap"], start, stop), [out], [l, r])
+
+    def iota(out, pat, base=0, cmul=0, small=True):
+        if small:
+            do("g", lambda: g.iota(out["ap"], pat, base, cmul, allow_small_or_imprecise_dtypes=True), [out], [])
+        else:
+            do("g", lambda: g.iota(out["ap"], pat, base, cmul), [out], [])
+
+    def sel(out, a, pat, op, base, cmul):
+        do("g", lambda: g.affine_select(out["ap"], a["ap"], pat, op, 0.0, base, cmul), [out], [a])
+
+    for q, k, name in (("s", "wk", "wks"), ("a", "fm", "fmi"), ("s", "lm", "lmi"), ("a", "tl", "tli"), ("s", "mo", "MO"),
+                       ("a", "sn", "sni"), ("s", "fr", "frs")):
+        dma(q, "ld" + k, v(name, ALL), {"ap": T[k][:]})
+    fill(v("ones", ALL), 1.0)
+    sel(v("bg0", ALL), v("ones", ALL), [[-16, 8], [0, 16]], O.is_ge, 0, 1)
+    sel(v("BG", ALL), v("bg0", ALL), [[16, 8], [0, 16]], O.is_ge, 15, -1)
+    iota(v("pi", S(0, 1)), [[0, 1]], 0, 1, small=False)
+    iota(v("nd", ALL), [[1, 16], [0, 16]])
+    iota(v("ci16", ALL), [[1, 16]])
+    iota(v("nm", ALL), [[0, 16], [1, 16]])
+    sel(v("ID", ALL), v("ones", ALL), [[-1, 128]], O.is_equal, 0, 1)
+    iota(v("jt", ALL), [[-1024, 16], [0, 16]])
+    iota(v("zi", ALL), [[1, 16], [0, 4]])
+    iota(v("ct16", ALL), [[16, 16]])
+    iota(v("cn16", ALL), [[1024, 4], [16, 4]])
+    iota(v("rt", ALL, ALL), [[256, 4], [0, 16]], 2048)
+    sel(v("TSs", ALL), v("BG", ALL), [[1, 128]], O.is_gt, 0, -1)
+    iota(v("itab", ALL), [[0, 4], [256, 16], [0, 64]])
+    fill(v("LU", ALL, ALL), 0.0)
+    fill(v("LV", ALL, ALL), 0.0)
+    fill(v("EX", ALL, ALL), 0.0)
+    cp(v("wkf", ALL), v("wks", ALL))
+    ts(v("nwk", ALL), v("wkf", ALL), -1.0, O.mult)
+    mp = [v("mp0", ALL), v("mp1", ALL)]
+    act(mp[0], v("fmi", ALL), bias=255.0, scale=-1.0)
+    for x in range(16):
+        ts(v("LU", x, S(x, None, 16)), v("BG", S(x, None, 16)), v("nwk", S(0, 1)), O.mult)
+        act(v("LV", x, S(x, None, 16)), v("BG", S(x, None, 16)), scale=v("nwk", S(1, 2)))
+    ts(v("WU", ALL), v("BG", ALL), v("wkf", S(0, 1)), O.mult)
+    ts(v("WV", ALL), v("BG", ALL), v("wkf", S(1, 2)), O.mult)
+    fill(v("c255", ALL), 255.0)
+    act(v("LM", S(16, 1040)), v("lmi", ALL), bias=255.0, scale=-1.0)
+    ts(v("pm", S(0, 1)), v("pi", S(0, 1)), 15, O.bitwise_and)
+    cp(v("pmf", S(0, 1)), v("pm", S(0, 1)))
+    pmf = v("pmf", S(0, 1))
+    ts(v("kr", ALL), v("nd", ALL), pmf, O.is_equal, v("wkf", S(2, 3)), O.mult)
+    mm(v("PK", S(0, 256)), v("BG", ALL), v("kr", ALL), True, True)
+    cp(v("kpat", ALL), v("PK", S(0, 256)))
+    ts(v("repa", ALL), v("ci16", ALL), 0.0, O.mult, pmf, O.add)
+    cp(v("repb", ALL), v("ci16", ALL))
+
+    def late_constants():
+        for x in range(16):
+            act(v("EX", x, S(x, None, 16)), v("BG", S(x, None, 16)), scale=-BIG)
+        ts(v("nI", ALL), v("ID", ALL), -1.0, O.mult)
+
+    def later_constants():
+        cp(v("IDf", ALL), v("ID", ALL))
+        ts(v("nIf", ALL), v("ID", ALL), -1.0, O.mult)
+        cp(v("BGf", ALL), v("BG", ALL))
+        tt(v("TSf", ALL), v("BGf", ALL), v("IDf", ALL), O.subtract)
+        ts(v("MD", ALL), v("nm", ALL), pmf, O.is_equal)
+        tt(v("TSf", ALL), v("TSf", ALL), v("TSs", ALL), O.subtract)
+        ts(v("zc", ALL), v("zi", ALL), 8192.0, O.mult, 15 * BIG + 2048, O.add)
+        ts(v("eq", ALL), v("nm", ALL), 0.0, O.mult, pmf, O.is_equal)
+        ts(v("lane", ALL), v("ct16", ALL), pmf, O.add)
+        for r in range(2):
+            ts(v("sd", r, ALL), v("lane", ALL), 1024.0, O.add)
+        ts(v("dl", ALL), v("lane", ALL), 1040.0, O.add)
+        ts(v("ds", ALL), v("lane", ALL), 6144.0, O.add)
+        ts(v("ln8", ALL), v("lane", ALL), 8192.0, O.add)
+        ts(v("nt", ALL), v("cn16", ALL), pmf, O.add)
+        fill(v("cbig", ALL), BIG)
+        ts(v("TS", ALL), v("ID", ALL), -2048.0, O.mult)
+        tt(v("TS", ALL), v("TS", ALL), v("TSs", ALL), O.add)
+
+    far = [d for d in T.cores if d != core and topo.chip(d) != topo.chip(core)]
+    near = [d for d in T.cores if d != core and topo.chip(d) == topo.chip(core)]
+    lines, used = {}, set()
+    for i, d in enumerate(far):
+        e = topo.engines(core, d)
+        lines[d] = e[i * 4:i * 4 + 4]
+        used.update(e)
+    for i, d in enumerate(near):
+        lines[d] = [x for x in topo.engines(core, d) if x not in used][i * 8:i * 8 + 8]
+    assert sum(len(x) for x in lines.values()) == 16
+    for t in range(4):
+        a, b = t * 160, t * 160 + rank * 40
+        note(None, "ar%d" % t, 16, [v("rx", S(a, b)), v("rx", S(b + 40, a + 160))], [])
+
+    def send(t):
+        r = [v("se", S(T.rank_of(d) * 256, T.rank_of(d) * 256 + 40)) for d in far + near]
+        wait("g", hazards("g", [], r))
+        tr = []
+        for d in far + near:
+            rid, pid = topo.addr(d)[:2]
+            a, b = T.rank_of(d) * 256, t * 160 + rank * 40
+            tr.append(RemoteDMATransfer(dst_ids=[DstId(rid=rid, pnc=pid)], dma_engine_mask=sum(1 << e for e in lines[d]),
+                                        remote_sem=T.sem["ar%d" % t], src=T.se[:, a:a + 40], dst=T.rx[:, b:b + 40]))
+        g.remote_dma_fused(tr, local_sem=T.sem.st)
+        note("g", "st", 16, [], r)
+
+    def front_sums(m):
+        for k, (L, W) in enumerate((("LU", "WU"), ("LV", "WV"))):
+            o = v("PU0", S(16 * k, 16 * k + 16))
+            mm(o, v(W, ALL), v("c255", S(0, 16)), True, False)
+            for x in range(16):
+                mm(o, v(L, x, ALL), v(m["n"], S(x, None, 16)), False, x == 15)
+
+    def places1():
+        cp(v("uvi", ALL), v("PU0", S(0, 32)))
+
+    def places2():
+        ts(v("uvm", ALL), v("uvi", ALL), 4095, O.bitwise_and)
+
+    def places3():
+        cp(v("uvf", ALL), v("uvm", S(0, 16)))
+        tt(v("uvs", ALL), v("uvm", S(0, 16)), v("uvm", S(16, 32)), O.mult)
+        ts(v("Aw", ALL), v("uvs", ALL), 5, O.arith_shift_right, 4095, O.bitwise_and)
+        tt(v("kt", ALL), ind(v("uvf", ALL), v("repa", ALL)), v("kpat", ALL), O.mult)
+        cp(v("Awf", ALL), v("Aw", ALL))
+
+    def places4():
+        tt(v("cc", ALL), ind(v("Awf", ALL), v("repa", ALL)), v("kt", ALL), O.add)
+        ts(v("cm", ALL), v("cc", ALL), 1023, O.bitwise_and)
+        cp(v("co", ALL), v("cm", ALL))
+
+    LMt, TLt, SNt = v("LM", S(16, 1040)), v("TL", S(16, 1040)), v("SN", S(2048, 6144))
+    front_sums(mp[0])
+    places1()
+    places2()
+    places3()
+    places4()
+    late_constants()
+    cp(TLt, v("tli", ALL))
+
+    for t in range(4):
+        m, n = mp[t % 2], mp[(t + 1) % 2]
+        A = list(range(16 - NACT, 16))
+
+        def look(j):
+            return ind(LMt, v("co", S(16 * j, 16 * j + 16)))
+
+        def own(j):
+            tt(v("V", S(256 * j, 256 * j + 256)), look(j), m, O.is_lt)
+
+        def diff(k):
+            gb_ = v(("ga", "gb")[(k // 2) % 2], S(256 * (k % 2), 256 * (k % 2) + 256))
+            act(gb_, look(A[k]), F.Copy)
+            o = v("PU%d" % ((k + 1) % 2), S(0, 256))
+            mm(o, v("ID", ALL), m, True, False)
+            mm(o, v("nI", ALL), gb_, False, True)
+
+        def excess(k):
+            act(v("V", S(256 * A[k], 256 * A[k] + 256)), v("PU%d" % ((k + 1) % 2), S(0, 256)), F.Relu)
+
+        def tally(a, b, last=False):
+            for x in range(16):
+                mm(v("PK", S(16 * a, 16 * b)), v("EX", x, ALL), v("V", S(256 * a + x, 256 * b, 16)), False, last and x == 15)
+
+        mm(v("PK", S(0, 256)), v("ID", ALL), v("jt", ALL), True, False)
+        diff(0)
+        diff(1)
+        for j in range(16 - NACT):
+            own(j)
+        for k in range(2, NACT):
+            excess(k - 2)
+            diff(k)
+            if k == 4:
+                tally(0, 4)
+        for k in range(NACT - 2, NACT):
+            excess(k)
+        if t == 0:
+            later_constants()
+        else:
+            cp(ind(v("TL", ALL), v("oL16", ALL)), v("wt", ALL))
+        if t < 3:
+            a = 160 if t else 0
+            act(v("ct", S(a, 256)), v("TL", S(16 + a, 272)), F.Copy)
+        tally(4, 8)
+        tally(16 - NACT, 16)
+        tally(8, 16 - NACT, True)
+        tt(v("ka", ALL), v("cm", ALL), v("PK", S(0, 256)), O.subtract)
+        tt(v("kc", S(0, 128)), v("ka", S(0, 128)), v("ka", S(128, 256)), O.min)
+        tt(v("ka", S(0, 64)), v("kc", S(0, 64)), v("kc", S(64, 128)), O.min)
+        tt(v("kc", S(0, 32)), v("ka", S(0, 32)), v("ka", S(32, 64)), O.min)
+        tt(v("k1", ALL), v("kc", S(0, 16)), v("kc", S(16, 32)), O.min)
+        ts(v("gi", ALL), v("k1", ALL), 1023, O.bitwise_and)
+        cp(v("g16", ALL), v("gi", ALL))
+        cp(v("tg", ALL), ind(TLt, v("g16", ALL)))
+        tt(v("ql", ALL), ind(LMt, v("g16", ALL)), m, O.subtract)
+
+        def pick(k):
+            act(v("Y", S(1024 * k, 1024 * k + 1024)), ind(v("MO", ALL), v("tg", S(64 * k, 64 * k + 64))), F.Copy)
+
+        def products(k):
+            X = "PX%d" % (k % 2)
+            for i in range(16):
+                mm(v(X, S(64 * i, 64 * i + 64)), v("nI", ALL), v("ql", S(64 * k, 64 * k + 64)), True, False)
+                mm(v(X, S(64 * i, 64 * i + 64)), v("nI", ALL), v("Y", S(1024 * k + i, 1024 * k + 1024, 16)), False, True)
+
+        def clip(k):
+            act(v("P", S(1024 * k, 1024 * k + 1024)), v("PX%d" % (k % 2), ALL), F.Relu, bias=255.0)
+
+        def hsum(k):
+            for z, (L, W) in enumerate((("LU", "WU"), ("LV", "WV"))):
+                o = v("PU%d" % (k % 2), S(64 * z, 64 * z + 64))
+                mm(o, v(W, ALL), v("c255", ALL), True, False)
+                for x in range(16):
+                    mm(o, v(L, x, ALL), v("P", S(1024 * k + x, 1024 * k + 1024, 16)), False, x == 15)
+
+        def hash_(k):
+            K, b = S(64 * k, 64 * k + 64), k % 2
+            d, e = S(64 * b, 64 * b + 64), 128 * b
+            cp(v("hi", S(e, e + 128)), v("PU%d" % b, S(0, 128)))
+            ts(v("hm", S(e, e + 128)), v("hi", S(e, e + 128)), 4095, O.bitwise_and)
+            tt(v("hs", d), v("hm", S(e, e + 64)), v("hm", S(e + 64, e + 128)), O.mult)
+            ts(v("ha", d), v("hs", d), 5, O.arith_shift_right, 4095, O.bitwise_and)
+            tt(v("hb", d), v("ha", d), v("hm", S(e, e + 64)), O.add)
+            ts(v("hc", K), v("hb", d), 4095, O.bitwise_and)
+            cp(v("h16", K), v("hc", K))
+
+        def seen(k):
+            K, n1 = S(64 * k, 64 * k + 64), SPLIT[k]
+            R = S(1024 * k, 1024 * k + 16 * n1)
+            tt(v("M", R), ind(SNt, v("h16", S(64 * k, 64 * k + n1))), v("P", R), O.not_equal)
+            tt(v("zk", K), v("hc", K), v("zc", ALL), O.add)
+
+        def seen2(k):
+            n1 = SPLIT[k]
+            if n1 < 64:
+                R, z = S(1024 * k + 16 * n1, 1024 * k + 1024), 1024 - 16 * n1
+                act(v("Y", R), ind(SNt, v("h16", S(64 * k + n1, 64 * k + 64))), F.Copy)
+                mm(v("PK", S(0, z)), v("ID", ALL), v("Y", R), True, False)
+                mm(v("PK", S(0, z)), v("nI", ALL), v("P", R), False, True)
+                act(v("M", R), v("PK", S(0, z)), F.Abs)
+
+        def unequal(k):
+            o = v("PU%d" % (k % 2), S(128, 192))
+            mm(o, v("BG", ALL), v("cbig", ALL), True, False)
+            for x in range(16):
+                mm(o, v("EX", x, ALL), v("M", S(1024 * k + x, 1024 * k + 1024, 16)), False, x == 15)
+
+        def keep(k):
+            a = 64 * k
+            tt(v("kb", S(a, a + 64)), v("PU%d" % (k % 2), S(128, 192)), v("zk", S(a, a + 64)), O.max)
+
+        def least(k):
+            a = 64 * k
+            tt(v("kd", S(a, a + 32)), v("kb", S(a, a + 32)), v("kb", S(a + 32, a + 64)), O.min)
+            tt(v("kb", S(a, a + 16)), v("kd", S(a, a + 16)), v("kd", S(a + 16, a + 32)), O.min)
+            tt(v("kd", S(a, a + 8)), v("kb", S(a, a + 8)), v("kb", S(a + 8, a + 16)), O.min)
+            tt(v("kz", S(4 * k, 4 * k + 4)), v("kd", S(a, a + 4)), v("kd", S(a + 4, a + 8)), O.min)
+
+        pick(0)
+        products(0)
+        pick(1)
+        products(1)
+        clip(0)
+        pick(2)
+        if t < 3:
+            tt(v("ya", ALL), ind(v("Awf", ALL), v("repb", ALL)), v("MD", ALL), O.mult)
+        if 0 < t < 3:
+            ts(v("tla", ALL), v("xi", ALL), 12, O.arith_shift_right, 4095, O.bitwise_and)
+            ts(v("cia", ALL), v("xi", ALL), 8, O.arith_shift_right, 15, O.bitwise_and)
+            tt(v("tmi", ALL), v("TL", S(16, 176)), v("inv", ALL), O.mult)
+            ts(v("eq", S(0, 160)), v("cia", ALL), pmf, O.is_equal)
+            tt(v("ct", S(0, 160)), v("tla", ALL), v("tmi", ALL), O.add)
+        ts(v("nfb", ALL), v("k1", ALL), 16384.0, O.is_ge, float(TOP), O.mult)
+        ts(v("nk0", ALL), v("k1", ALL), 16384.0, O.is_lt, 65536.0, O.mult)
+        fill(v("se", S(0, 40)), -0.25)
+        ts(v("nk0", ALL), v("nk0", ALL), 16.0, O.add)
+        fill(v("se", S(256, 296)), -0.25)
+        tt(v("nk1", ALL), v("cm", S(0, 16)), v("nk0", ALL), O.add)
+        fill(v("se", S(512, 552)), -0.25)
+        tt(v("nk", ALL), v("nk1", ALL), v("ln8", ALL), O.min)
+        fill(v("se", S(768, 808)), -0.25)
+        if t < 3:
+            mm(v("PK", S(256, 512)), v("BGf", ALL), v("ya", ALL), True, False)
+            mm(v("PK", S(256, 512)), v("nIf", ALL), v("ct", ALL), False, True)
+        hsum(0)
+        clip(1)
+        if t > 0:
+            cp(ind(v("SN", ALL), v("oS16", ALL)), v("pc", ALL))
+        else:
+            ts(SNt, v("sni", ALL), -1.0, O.mult, 255.0, O.add)
+        hash_(0)
+        if t < 3:
+            tt(v("wd", ALL), v("PK", S(256, 512)), v("eq", ALL), O.mult)
+        products(2)
+        hsum(1)
+        pick(3)
+        seen(0)
+        clip(2)
+        hash_(1)
+        products(3)
+        if t < 3:
+            mm(v("PK", S(0, 256)), v("IDf", ALL), v("ct", ALL), True, False)
+            mm(v("PK", S(0, 256)), v("IDf", ALL), v("wd", ALL), False, True)
+        unequal(0)
+        hsum(2)
+        seen(1)
+        clip(3)
+        if t < 3:
+            act(v("wt", ALL), v("PK", S(0, 256)), F.Copy)
+        keep(0)
+        hash_(2)
+        unequal(1)
+        hsum(3)
+        seen2(2)
+        seen(2)
+        keep(1)
+        act(v("t4", ALL), ind(TLt, v("g16", ALL)), scale=4096.0)
+        hash_(3)
+        seen2(3)
+        unequal(2)
+        seen(3)
+        least(0)
+        least(1)
+        keep(2)
+        least(2)
+        if t == 0:
+            act(v("frs", ALL), v("frs", ALL), bias=255.0, scale=-1.0)
+        act(v(n["n"], S(160, 256)), v("frs", S(t * 256 + 160, t * 256 + 256)), F.Copy)
+        unequal(3)
+        keep(3)
+        least(3)
+        tt(v("k3", ALL), v("kz", ALL), v("nfb", ALL), O.max)
+        ts(v("rr", ALL), v("k3", ALL), TOP + 3, O.bitwise_and)
+        ts(v("n0", ALL), v("k3", ALL), 7, O.arith_shift_right, 960, O.bitwise_and)
+        for r in range(4):
+            ts(v("D4", r, ALL), v("rr", ALL), float(r), O.is_equal)
+
+        def pr(r0, r1, c0):
+            return v("PM", S(r0, r1), S(c0, 16))
+        mm(pr(0, 4, 0), v("TS", ALL), v("D4", ALL, ALL), True, False)
+        mm(pr(0, 4, 0), v("ID", ALL), v("rt", ALL, ALL), False, False)
+        for s in range(1, 16):
+            mm(pr(0, 4, s), v("BG", ALL), v("D4", ALL, S(0, 16 - s)), False, s == 15)
+        tt(v("n1", ALL), v("n0", ALL), v("nt", ALL), O.add)
+        cp(v("n16", ALL), v("n1", ALL))
+        act(v("pc", ALL), ind(v("P", ALL), v("n16", ALL)), F.Copy)
+        tt(v("t1", ALL), ind(v("itab", ALL), v("n16", ALL)), v("t4", ALL), O.add)
+        tt(v("o1", ALL, ALL), pr(0, 2, 0), v("sd", ALL, ALL), O.min)
+        tt(v("o2", ALL, ALL), pr(2, 4, 0), v("o1", ALL, ALL), O.min)
+        tt(v("o3", ALL), v("o2", 0, ALL), v("o2", 1, ALL), O.min)
+        cp(v("s16", ALL), v("o3", ALL))
+        tt(ind(v("se", ALL), v("s16", ALL)), v("t1", ALL), v("pc", ALL), O.add)
+        send(t)
+        q = S(t * 160, t * 160 + 160)
+        act(v("rx", S(t * 160 + rank * 40, t * 160 + rank * 40 + 40)), v("se", S(rank * 256, rank * 256 + 40)), F.Copy)
+        ts(v("hk", ALL), v("k3", ALL), TOP + 8191, O.bitwise_and)
+        tt(v("key", ALL), v("hk", ALL), v("nk", ALL), O.min)
+        tt(v("ya", ALL), ind(v("key", ALL), v("repb", ALL)), v("MD", ALL), O.mult)
+        mm(v("PK", S(0, 256)), v("BGf", ALL), v("ya", ALL), True, True)
+        mm(v("PK", S(256, 512)), v("TSf", ALL), v("ya", ALL), True, True)
+        cp(v("kw", ALL), v("PK", S(0, 256)))
+        act(v("kdf", ALL), v("PK", S(256, 512)), F.Copy)
+        act(v("inv", ALL), v("rx", q), F.Relu, scale=-4.0)
+        for c in range(15):
+            ts(v("E", c, S(0, 240 - 16 * c)), v("kw", S(16 * c + 16, 256)), v("key", S(c, c + 1)), O.is_equal)
+            if c == 3:
+                tt(v("E", 15, ALL), ind(v("key", ALL), v("repb", ALL)), v("kdf", ALL), O.is_equal)
+        mm(v("PK", S(0, 256)), v("BG", ALL), v("E", 15, ALL), True, False)
+        for c in range(15):
+            mm(v("PK", S(16 * c + 16, 256)), v("BG", ALL), v("E", c, S(0, 240 - 16 * c)), False, c == 14)
+        act(v("dub", ALL), v("PK", S(0, 256)), F.Copy)
+        for x in range(16):
+            mm(v("PM", 20, ALL), v("EX", x, ALL), v("dub", S(x, None, 16)), x == 0, x == 15)
+        cp(v("xi", ALL), v("rx", q))
+        tt(v("ri", ALL), v("frs", S(t * 256, t * 256 + 160)), v("inv", ALL), O.mult)
+        ts(v("pa", ALL), v("xi", ALL), 255, O.bitwise_and)
+        tt(v(n["n"], S(0, 160)), v("pa", ALL), v("ri", ALL), O.add)
+        if t < 3:
+            front_sums(n)
+        else:
+            act(v("ga", S(0, 256)), n, bias=255.0, scale=-1.0)
+            o2 = dma("s", "of", {"ap": T.yf[:]}, v("ga", S(0, 256)))
+        ts(v("los", ALL), v("PM", 20, ALL), -1.0, O.is_le, 65536.0, O.mult)
+        if t < 3:
+            places1()
+        tt(v("kl", ALL), v("key", ALL), v("los", ALL), O.add)
+        if t < 3:
+            places2()
+        tt(v("oL", ALL), v("kl", ALL), v("dl", ALL), O.min)
+        if t < 3:
+            places3()
+        cp(v("oL16", ALL), v("oL", ALL))
+        cp(ind(v("LM", ALL), v("oL16", ALL)), m)
+        if t < 3:
+            places4()
+            tt(v("oS", ALL), v("kl", ALL), v("ds", ALL), O.min)
+            cp(v("oS16", ALL), v("oS", ALL))
+        else:
+            act(v("Y", S(0, 1024)), LMt, bias=255.0, scale=-1.0)
+            o1 = dma("s", "ol", {"ap": T.yl[:]}, v("Y", S(0, 1024)))
+            wait("s", [o1])
+            wait("s", [o2])
+    for tag in ("st", "v", "a", "p", "g"):
+        wait("g", [[i for i, o in enumerate(ops) if o[0] == tag][-1]])

@@ -13,13 +13,13 @@ SHAPES = {
     "sd": ([2, 16], F32), "c255": ([64], B), "cbig": ([64], B), "itab": ([4096], B), "mp0": ([256], B), "mp1": ([256], B),
     "uvi": ([32], I32), "uvm": ([32], I32), "kt": ([256], F32), "cc": ([256], I32), "cm": ([256], I32), "co": ([256], U16),
     "V": ([4096], B), "ga": ([512], B), "gb": ([512], B), "ka": ([256], F32), "kc": ([256], F32), "ql": ([256], B),
-    "tg": ([256], U16), "t4": ([256], F32), "ya": ([256], F32), "ct": ([256], F32), "eq": ([256], F32), "wd": ([256], F32),
-    "wt": ([256], F32), "tla": ([160], I32), "cia": ([160], I32), "tmi": ([160], F32), "Y": ([4096], B), "P": ([4096], B),
-    "hi": ([256], I32), "hm": ([256], I32), "hs": ([128], I32), "ha": ([128], I32), "hb": ([128], I32), "hc": ([256], I32),
-    "h16": ([256], U16), "zk": ([256], F32), "M": ([4096], B), "kb": ([256], F32), "kd": ([256], F32), "D4": ([4, 16], B),
-    "t1": ([256], F32), "pc": ([256], F32), "o1": ([2, 16], F32), "o2": ([2, 16], F32), "kw": ([256], U16), "kdf": ([256], F32),
-    "E": ([16, 256], B), "dub": ([256], B), "xi": ([160], I32), "pa": ([160], I32), "inv": ([160], B), "ri": ([160], B),
-    "se": ([1280], F32), "rx": ([640], F32),
+    "tg": ([256], U16), "t4": ([256], F32), "ya": ([256], F32), "yb": ([256], F32), "ct": ([256], F32), "eq": ([256], F32),
+    "wd": ([256], F32), "wt": ([256], F32), "tla": ([160], I32), "cia": ([160], I32), "tmi": ([160], F32), "Y": ([4096], B),
+    "P": ([4096], B), "hi": ([256], I32), "hm": ([256], I32), "hs": ([128], I32), "ha": ([128], I32), "hb": ([128], I32),
+    "hc": ([256], I32), "h16": ([256], U16), "zk": ([256], F32), "M": ([4096], B), "kb": ([256], F32), "kd": ([256], F32),
+    "D4": ([4, 16], B), "t1": ([256], F32), "pc": ([256], F32), "o1": ([2, 16], F32), "o2": ([2, 16], F32), "kw": ([256], U16),
+    "kdf": ([256], F32), "E": ([16, 256], B), "dub": ([256], B), "xi": ([160], I32), "pa": ([160], I32), "inv": ([160], B),
+    "ri": ([160], B), "se": ([1280], F32), "rx": ([640], F32),
 }
 SUB = {"sni": ("M", 0, 4096), "lmi": ("Y", 0, 1024), "fmi": ("ga", 0, 256), "bg0": ("gb", 0, 128)}
 for name, typ, names in (
@@ -36,7 +36,8 @@ SEMAPHORES = ["sv", "sa", "sp", "sg", "st", "ol", "of"] + ["ld" + k for k in LOA
 BIG = 131072.0
 TOP = 2097152
 NACT = 6
-SPLIT = (64, 64, 32, 32)
+MID = 12
+SPLIT = (64, 64, 32, 48)
 
 
 def rank_program(g, core, T, topo):
@@ -223,6 +224,7 @@ def rank_program(g, core, T, topo):
         ts(v("ln8", ALL), v("lane", ALL), 8192.0, O.add)
         ts(v("nt", ALL), v("cn16", ALL), pmf, O.add)
         fill(v("cbig", ALL), BIG)
+        fill(v("E", 0, S(0, 16)), 0.0)
         ts(v("TS", ALL), v("ID", ALL), -2048.0, O.mult)
         tt(v("TS", ALL), v("TS", ALL), v("TSs", ALL), O.add)
 
@@ -261,28 +263,28 @@ def rank_program(g, core, T, topo):
 
     def places1():
         cp(v("uvi", ALL), v("PU0", S(0, 32)))
-
-    def places2():
         ts(v("uvm", ALL), v("uvi", ALL), 4095, O.bitwise_and)
-
-    def places3():
         cp(v("uvf", ALL), v("uvm", S(0, 16)))
         tt(v("uvs", ALL), v("uvm", S(0, 16)), v("uvm", S(16, 32)), O.mult)
         ts(v("Aw", ALL), v("uvs", ALL), 5, O.arith_shift_right, 4095, O.bitwise_and)
         tt(v("kt", ALL), ind(v("uvf", ALL), v("repa", ALL)), v("kpat", ALL), O.mult)
         cp(v("Awf", ALL), v("Aw", ALL))
 
-    def places4():
+    def places2():
         tt(v("cc", ALL), ind(v("Awf", ALL), v("repa", ALL)), v("kt", ALL), O.add)
         ts(v("cm", ALL), v("cc", ALL), 1023, O.bitwise_and)
         cp(v("co", ALL), v("cm", ALL))
+
+    def weave(a, b):
+        for z in range(max(len(a), len(b))):
+            for y in (a, b):
+                if z < len(y):
+                    y[z]()
 
     LMt, TLt, SNt = v("LM", S(16, 1040)), v("TL", S(16, 1040)), v("SN", S(2048, 6144))
     front_sums(mp[0])
     places1()
     places2()
-    places3()
-    places4()
     late_constants()
     cp(TLt, v("tli", ALL))
 
@@ -318,8 +320,10 @@ def rank_program(g, core, T, topo):
         for k in range(2, NACT):
             excess(k - 2)
             diff(k)
-            if k == 4:
+            if k == 2:
                 tally(0, 4)
+            if k == 4:
+                tally(4, 8)
         for k in range(NACT - 2, NACT):
             excess(k)
         if t == 0:
@@ -329,9 +333,8 @@ def rank_program(g, core, T, topo):
         if t < 3:
             a = 160 if t else 0
             act(v("ct", S(a, 256)), v("TL", S(16 + a, 272)), F.Copy)
-        tally(4, 8)
-        tally(16 - NACT, 16)
-        tally(8, 16 - NACT, True)
+        tally(8, MID)
+        tally(MID, 16, True)
         tt(v("ka", ALL), v("cm", ALL), v("PK", S(0, 256)), O.subtract)
         tt(v("kc", S(0, 128)), v("ka", S(0, 128)), v("ka", S(128, 256)), O.min)
         tt(v("ka", S(0, 64)), v("kc", S(0, 64)), v("kc", S(64, 128)), O.min)
@@ -339,17 +342,20 @@ def rank_program(g, core, T, topo):
         tt(v("k1", ALL), v("kc", S(0, 16)), v("kc", S(16, 32)), O.min)
         ts(v("gi", ALL), v("k1", ALL), 1023, O.bitwise_and)
         cp(v("g16", ALL), v("gi", ALL))
-        cp(v("tg", ALL), ind(TLt, v("g16", ALL)))
+        cp(v("tg", S(0, 64)), ind(TLt, v("g16", S(0, 4))))
+        cp(v("tg", S(64, 256)), ind(TLt, v("g16", S(4, 16))))
         tt(v("ql", ALL), ind(LMt, v("g16", ALL)), m, O.subtract)
 
         def pick(k):
             act(v("Y", S(1024 * k, 1024 * k + 1024)), ind(v("MO", ALL), v("tg", S(64 * k, 64 * k + 64))), F.Copy)
 
-        def products(k):
-            X = "PX%d" % (k % 2)
+        def minuend(k):
             for i in range(16):
-                mm(v(X, S(64 * i, 64 * i + 64)), v("nI", ALL), v("ql", S(64 * k, 64 * k + 64)), True, False)
-                mm(v(X, S(64 * i, 64 * i + 64)), v("nI", ALL), v("Y", S(1024 * k + i, 1024 * k + 1024, 16)), False, True)
+                mm(v("PX%d" % (k % 2), S(64 * i, 64 * i + 64)), v("nI", ALL), v("ql", S(64 * k, 64 * k + 64)), i % 8 == 0, False)
+
+        def products(k):
+            for i in range(16):
+                mm(v("PX%d" % (k % 2), S(64 * i, 64 * i + 64)), v("nI", ALL), v("Y", S(1024 * k + i, 1024 * k + 1024, 16)), False, i % 8 == 7)
 
         def clip(k):
             act(v("P", S(1024 * k, 1024 * k + 1024)), v("PX%d" % (k % 2), ALL), F.Relu, bias=255.0)
@@ -364,119 +370,107 @@ def rank_program(g, core, T, topo):
         def hash_(k):
             K, b = S(64 * k, 64 * k + 64), k % 2
             d, e = S(64 * b, 64 * b + 64), 128 * b
-            cp(v("hi", S(e, e + 128)), v("PU%d" % b, S(0, 128)))
-            ts(v("hm", S(e, e + 128)), v("hi", S(e, e + 128)), 4095, O.bitwise_and)
-            tt(v("hs", d), v("hm", S(e, e + 64)), v("hm", S(e + 64, e + 128)), O.mult)
-            ts(v("ha", d), v("hs", d), 5, O.arith_shift_right, 4095, O.bitwise_and)
-            tt(v("hb", d), v("ha", d), v("hm", S(e, e + 64)), O.add)
-            ts(v("hc", K), v("hb", d), 4095, O.bitwise_and)
-            cp(v("h16", K), v("hc", K))
+            return [lambda: cp(v("hi", S(e, e + 128)), v("PU%d" % b, S(0, 128))),
+                    lambda: ts(v("hm", S(e, e + 128)), v("hi", S(e, e + 128)), 4095, O.bitwise_and),
+                    lambda: tt(v("hs", d), v("hm", S(e, e + 64)), v("hm", S(e + 64, e + 128)), O.mult),
+                    lambda: ts(v("ha", d), v("hs", d), 5, O.arith_shift_right, 4095, O.bitwise_and),
+                    lambda: tt(v("hb", d), v("ha", d), v("hm", S(e, e + 64)), O.add),
+                    lambda: ts(v("hc", K), v("hb", d), 4095, O.bitwise_and),
+                    lambda: cp(v("h16", K), v("hc", K))]
 
         def seen(k):
-            K, n1 = S(64 * k, 64 * k + 64), SPLIT[k]
+            n1 = SPLIT[k]
             R = S(1024 * k, 1024 * k + 16 * n1)
             tt(v("M", R), ind(SNt, v("h16", S(64 * k, 64 * k + n1))), v("P", R), O.not_equal)
-            tt(v("zk", K), v("hc", K), v("zc", ALL), O.add)
+
+        def rows(k):
+            K = S(64 * k, 64 * k + 64)
+            return [lambda: tt(v("zk", K), v("hc", K), v("zc", ALL), O.add)]
 
         def seen2(k):
             n1 = SPLIT[k]
-            if n1 < 64:
-                R, z = S(1024 * k + 16 * n1, 1024 * k + 1024), 1024 - 16 * n1
-                act(v("Y", R), ind(SNt, v("h16", S(64 * k + n1, 64 * k + 64))), F.Copy)
-                mm(v("PK", S(0, z)), v("ID", ALL), v("Y", R), True, False)
-                mm(v("PK", S(0, z)), v("nI", ALL), v("P", R), False, True)
-                act(v("M", R), v("PK", S(0, z)), F.Abs)
+            R, o = S(1024 * k + 16 * n1, 1024 * k + 1024), v("PX%d" % (k % 2), S(0, 1024 - 16 * n1))
+            act(v("Y", R), ind(SNt, v("h16", S(64 * k + n1, 64 * k + 64))), F.Copy)
+            mm(o, v("ID", ALL), v("Y", R), True, False)
+            mm(o, v("nI", ALL), v("P", R), False, True)
+            act(v("M", R), o, F.Abs)
 
         def unequal(k):
-            o = v("PU%d" % (k % 2), S(128, 192))
+            o = v("PK", S(64 * k, 64 * k + 64))
             mm(o, v("BG", ALL), v("cbig", ALL), True, False)
             for x in range(16):
                 mm(o, v("EX", x, ALL), v("M", S(1024 * k + x, 1024 * k + 1024, 16)), False, x == 15)
 
-        def keep(k):
-            a = 64 * k
-            tt(v("kb", S(a, a + 64)), v("PU%d" % (k % 2), S(128, 192)), v("zk", S(a, a + 64)), O.max)
-
         def least(k):
             a = 64 * k
-            tt(v("kd", S(a, a + 32)), v("kb", S(a, a + 32)), v("kb", S(a + 32, a + 64)), O.min)
-            tt(v("kb", S(a, a + 16)), v("kd", S(a, a + 16)), v("kd", S(a + 16, a + 32)), O.min)
-            tt(v("kd", S(a, a + 8)), v("kb", S(a, a + 8)), v("kb", S(a + 8, a + 16)), O.min)
-            tt(v("kz", S(4 * k, 4 * k + 4)), v("kd", S(a, a + 4)), v("kd", S(a + 4, a + 8)), O.min)
+            return [lambda: tt(v("kb", S(a, a + 64)), v("PK", S(a, a + 64)), v("zk", S(a, a + 64)), O.max),
+                    lambda: tt(v("kd", S(a, a + 32)), v("kb", S(a, a + 32)), v("kb", S(a + 32, a + 64)), O.min),
+                    lambda: tt(v("kb", S(a, a + 16)), v("kd", S(a, a + 16)), v("kd", S(a + 16, a + 32)), O.min),
+                    lambda: tt(v("kd", S(a, a + 8)), v("kb", S(a, a + 8)), v("kb", S(a + 8, a + 16)), O.min),
+                    lambda: tt(v("kz", S(4 * k, 4 * k + 4)), v("kd", S(a, a + 4)), v("kd", S(a + 4, a + 8)), O.min)]
 
         pick(0)
+        minuend(0)
+        minuend(1)
         products(0)
         pick(1)
         products(1)
         clip(0)
         pick(2)
         if t < 3:
-            tt(v("ya", ALL), ind(v("Awf", ALL), v("repb", ALL)), v("MD", ALL), O.mult)
+            tt(v("yb", ALL), ind(v("Awf", ALL), v("repb", ALL)), v("MD", ALL), O.mult)
         if 0 < t < 3:
             ts(v("tla", ALL), v("xi", ALL), 12, O.arith_shift_right, 4095, O.bitwise_and)
             ts(v("cia", ALL), v("xi", ALL), 8, O.arith_shift_right, 15, O.bitwise_and)
             tt(v("tmi", ALL), v("TL", S(16, 176)), v("inv", ALL), O.mult)
             ts(v("eq", S(0, 160)), v("cia", ALL), pmf, O.is_equal)
             tt(v("ct", S(0, 160)), v("tla", ALL), v("tmi", ALL), O.add)
-        ts(v("nfb", ALL), v("k1", ALL), 16384.0, O.is_ge, float(TOP), O.mult)
-        ts(v("nk0", ALL), v("k1", ALL), 16384.0, O.is_lt, 65536.0, O.mult)
-        fill(v("se", S(0, 40)), -0.25)
-        ts(v("nk0", ALL), v("nk0", ALL), 16.0, O.add)
-        fill(v("se", S(256, 296)), -0.25)
-        tt(v("nk1", ALL), v("cm", S(0, 16)), v("nk0", ALL), O.add)
-        fill(v("se", S(512, 552)), -0.25)
-        tt(v("nk", ALL), v("nk1", ALL), v("ln8", ALL), O.min)
-        fill(v("se", S(768, 808)), -0.25)
-        if t < 3:
-            mm(v("PK", S(256, 512)), v("BGf", ALL), v("ya", ALL), True, False)
-            mm(v("PK", S(256, 512)), v("nIf", ALL), v("ct", ALL), False, True)
+        side = [lambda: ts(v("nfb", ALL), v("k1", ALL), 16384.0, O.is_ge, float(TOP), O.mult),
+                lambda: ts(v("nk0", ALL), v("k1", ALL), 16384.0, O.is_lt, 65536.0, O.mult),
+                lambda: fill(v("se", S(0, 40)), -0.25),
+                lambda: tt(v("nk1", ALL), v("cm", S(0, 16)), v("nk0", ALL), O.add),
+                lambda: fill(v("se", S(256, 296)), -0.25),
+                lambda: ts(v("nk0", ALL), v("nk1", ALL), 16.0, O.add),
+                lambda: fill(v("se", S(512, 552)), -0.25),
+                lambda: tt(v("nk", ALL), v("nk0", ALL), v("ln8", ALL), O.min),
+                lambda: fill(v("se", S(768, 808)), -0.25)]
         hsum(0)
         clip(1)
         if t > 0:
             cp(ind(v("SN", ALL), v("oS16", ALL)), v("pc", ALL))
         else:
             ts(SNt, v("sni", ALL), -1.0, O.mult, 255.0, O.add)
-        hash_(0)
-        if t < 3:
-            tt(v("wd", ALL), v("PK", S(256, 512)), v("eq", ALL), O.mult)
+        weave(hash_(0), [])
+        minuend(2)
         products(2)
         hsum(1)
         pick(3)
         seen(0)
         clip(2)
-        hash_(1)
+        weave(rows(0) + hash_(1), side)
+        minuend(3)
         products(3)
-        if t < 3:
-            mm(v("PK", S(0, 256)), v("IDf", ALL), v("ct", ALL), True, False)
-            mm(v("PK", S(0, 256)), v("IDf", ALL), v("wd", ALL), False, True)
         unequal(0)
         hsum(2)
         seen(1)
         clip(3)
-        if t < 3:
-            act(v("wt", ALL), v("PK", S(0, 256)), F.Copy)
-        keep(0)
-        hash_(2)
+        weave(rows(1) + least(0), hash_(2))
         unequal(1)
         hsum(3)
         seen2(2)
         seen(2)
-        keep(1)
         act(v("t4", ALL), ind(TLt, v("g16", ALL)), scale=4096.0)
-        hash_(3)
-        seen2(3)
+        weave(rows(2) + least(1), hash_(3))
         unequal(2)
+        seen2(3)
         seen(3)
-        least(0)
-        least(1)
-        keep(2)
-        least(2)
+        weave(rows(3), [])
+        weave(least(2), [])
         if t == 0:
             act(v("frs", ALL), v("frs", ALL), bias=255.0, scale=-1.0)
         act(v(n["n"], S(160, 256)), v("frs", S(t * 256 + 160, t * 256 + 256)), F.Copy)
         unequal(3)
-        keep(3)
-        least(3)
+        weave(least(3), [])
         tt(v("k3", ALL), v("kz", ALL), v("nfb", ALL), O.max)
         ts(v("rr", ALL), v("k3", ALL), TOP + 3, O.bitwise_and)
         ts(v("n0", ALL), v("k3", ALL), 7, O.arith_shift_right, 960, O.bitwise_and)
@@ -489,6 +483,9 @@ def rank_program(g, core, T, topo):
         mm(pr(0, 4, 0), v("ID", ALL), v("rt", ALL, ALL), False, False)
         for s in range(1, 16):
             mm(pr(0, 4, s), v("BG", ALL), v("D4", ALL, S(0, 16 - s)), False, s == 15)
+        if t < 3:
+            mm(v("PX0", S(0, 256)), v("BGf", ALL), v("yb", ALL), True, False)
+            mm(v("PX0", S(0, 256)), v("nIf", ALL), v("ct", ALL), False, True)
         tt(v("n1", ALL), v("n0", ALL), v("nt", ALL), O.add)
         cp(v("n16", ALL), v("n1", ALL))
         act(v("pc", ALL), ind(v("P", ALL), v("n16", ALL)), F.Copy)
@@ -505,20 +502,18 @@ def rank_program(g, core, T, topo):
         tt(v("key", ALL), v("hk", ALL), v("nk", ALL), O.min)
         tt(v("ya", ALL), ind(v("key", ALL), v("repb", ALL)), v("MD", ALL), O.mult)
         mm(v("PK", S(0, 256)), v("BGf", ALL), v("ya", ALL), True, True)
-        mm(v("PK", S(256, 512)), v("TSf", ALL), v("ya", ALL), True, True)
+        mm(v("PX1", S(0, 256)), v("TSf", ALL), v("ya", ALL), True, True)
         cp(v("kw", ALL), v("PK", S(0, 256)))
-        act(v("kdf", ALL), v("PK", S(256, 512)), F.Copy)
+        act(v("kdf", ALL), v("PX1", S(0, 256)), F.Copy)
         act(v("inv", ALL), v("rx", q), F.Relu, scale=-4.0)
         for c in range(15):
-            ts(v("E", c, S(0, 240 - 16 * c)), v("kw", S(16 * c + 16, 256)), v("key", S(c, c + 1)), O.is_equal)
-            if c == 3:
+            z = 16 if c == 0 else 0
+            ts(v("E", c, S(z, z + 240 - 16 * c)), v("kw", S(16 * c + 16, 256)), v("key", S(c, c + 1)), O.is_equal)
+            mm(v("PK", S(16 * c + 16 - z, 256)), v("BG", ALL), v("E", c, S(0, z + 240 - 16 * c)), c == 0, False)
+            if c == 7:
                 tt(v("E", 15, ALL), ind(v("key", ALL), v("repb", ALL)), v("kdf", ALL), O.is_equal)
-        mm(v("PK", S(0, 256)), v("BG", ALL), v("E", 15, ALL), True, False)
-        for c in range(15):
-            mm(v("PK", S(16 * c + 16, 256)), v("BG", ALL), v("E", c, S(0, 240 - 16 * c)), False, c == 14)
+        mm(v("PK", S(0, 256)), v("BG", ALL), v("E", 15, ALL), False, True)
         act(v("dub", ALL), v("PK", S(0, 256)), F.Copy)
-        for x in range(16):
-            mm(v("PM", 20, ALL), v("EX", x, ALL), v("dub", S(x, None, 16)), x == 0, x == 15)
         cp(v("xi", ALL), v("rx", q))
         tt(v("ri", ALL), v("frs", S(t * 256, t * 256 + 160)), v("inv", ALL), O.mult)
         ts(v("pa", ALL), v("xi", ALL), 255, O.bitwise_and)
@@ -528,19 +523,21 @@ def rank_program(g, core, T, topo):
         else:
             act(v("ga", S(0, 256)), n, bias=255.0, scale=-1.0)
             o2 = dma("s", "of", {"ap": T.yf[:]}, v("ga", S(0, 256)))
-        ts(v("los", ALL), v("PM", 20, ALL), -1.0, O.is_le, 65536.0, O.mult)
+        for x in range(16):
+            mm(v("PM", 20, ALL), v("EX", x, ALL), v("dub", S(x, None, 16)), x == 0, x == 15)
         if t < 3:
+            tt(v("wd", ALL), v("PX0", S(0, 256)), v("eq", ALL), O.mult)
+            mm(v("PX0", S(256, 512)), v("IDf", ALL), v("ct", ALL), True, False)
+            mm(v("PX0", S(256, 512)), v("IDf", ALL), v("wd", ALL), False, True)
+            act(v("wt", ALL), v("PX0", S(256, 512)), F.Copy)
             places1()
+        ts(v("los", ALL), v("PM", 20, ALL), -1.0, O.is_le, 65536.0, O.mult)
         tt(v("kl", ALL), v("key", ALL), v("los", ALL), O.add)
-        if t < 3:
-            places2()
         tt(v("oL", ALL), v("kl", ALL), v("dl", ALL), O.min)
-        if t < 3:
-            places3()
         cp(v("oL16", ALL), v("oL", ALL))
         cp(ind(v("LM", ALL), v("oL16", ALL)), m)
         if t < 3:
-            places4()
+            places2()
             tt(v("oS", ALL), v("kl", ALL), v("ds", ALL), O.min)
             cp(v("oS16", ALL), v("oS", ALL))
         else:

import numpy as np
from concourse.bass import DstId, RemoteDMATransfer
from concourse.mybir import AluOpType as O, ActivationFunctionType as F

B, I32, F32, U16 = "bfloat16", "int32", "float32", "uint16"
SHAPES = {
    "wks": ([3], I32), "tli": ([1024], I32), "frs": ([1024], B), "LM": ([1296], B), "TL": ([1296], F32), "MO": ([4096], B),
    "SN": ([6400], B), "ones": ([128], B), "BG": ([128], B), "ID": ([128], B), "TSs": ([128], B), "TS": ([128], B),
    "nI": ([128], B), "IDf": ([128], F32), "nIf": ([128], F32), "BGf": ([128], F32), "TSf": ([128], F32), "LU": ([16, 128], B),
    "LV": ([16, 128], B), "EX": ([16, 128], B), "WU": ([128], B), "WV": ([128], B), "wkf": ([3], F32), "nwk": ([3], F32),
    "pi": ([8], I32), "pm": ([8], I32), "pmf": ([8], F32), "nm": ([256], F32), "nd": ([256], F32), "MD": ([256], F32),
    "kr": ([256], B), "kpat": ([256], F32), "jt": ([256], B), "zi": ([64], F32), "zc": ([64], F32), "rt": ([4, 16], B),
    "sd": ([2, 16], F32), "c255": ([64], B), "cbig": ([64], B), "itab": ([4096], B), "mp0": ([256], B), "mp1": ([256], B),
    "uvi": ([32], I32), "uvm": ([32], I32), "kt": ([256], F32), "cc": ([256], I32), "cm": ([256], I32), "co": ([256], U16),
    "V": ([4096], B), "ga": ([512], B), "gb": ([512], B), "ka": ([256], F32), "kc": ([256], F32), "ql": ([256], B),
    "tg": ([256], U16), "t4": ([256], F32), "ya": ([256], F32), "yb": ([256], F32), "ct": ([256], F32), "eq": ([256], F32),
    "wd": ([256], F32), "wt": ([256], F32), "tla": ([160], I32), "cia": ([160], I32), "tmi": ([160], F32), "Y": ([4096], B),
    "P": ([4096], B), "hi": ([256], I32), "hm": ([256], I32), "hs": ([128], I32), "ha": ([128], I32), "hb": ([128], I32),
    "hc": ([256], I32), "h16": ([256], U16), "zk": ([256], F32), "M": ([4096], B), "kb": ([256], F32), "kd": ([256], F32),
    "D4": ([4, 16], B), "t1": ([256], F32), "pc": ([256], F32), "o1": ([2, 16], F32), "o2": ([2, 16], F32), "kw": ([256], U16),
    "kdf": ([256], F32), "E": ([16, 256], B), "dub": ([256], B), "xi": ([160], I32), "pa": ([160], I32), "inv": ([160], B),
    "ri": ([160], B), "se": ([1280], F32), "rx": ([640], F32),
}
SUB = {"sni": ("M", 0, 4096), "lmi": ("Y", 0, 1024), "fmi": ("ga", 0, 256), "bg0": ("gb", 0, 128)}
for name, typ, names in (
        ("F16", F32, "nfb nk0 nk1 nk key los kl oL oS o3 lane dl ds ln8 ci16 ct16 cn16 uvf Awf kz"),
        ("N16", I32, "uvs Aw k1 gi k3 n0 n1 rr hk nt"), ("H16", U16, "g16 n16 s16 oL16 oS16 repa repb")):
    names = names.split()
    SHAPES[name] = ([16 * len(names)], typ)
    SUB.update({k: (name, 16 * i, 16) for i, k in enumerate(names)})
PS = {"PX0": [1024], "PX1": [1024], "PU0": [512], "PU1": [512], "PK": [512], "PM": [32, 16]}
SCRATCH = {k: ("sbuf", [128] + s, d) for k, (s, d) in SHAPES.items()}
SCRATCH.update({k: ("psum", [128] + s, F32) for k, s in PS.items()})
LOADS = ["wk", "fm", "lm", "tl", "mo", "sn", "fr"]
SEMAPHORES = ["sv", "sa", "sp", "sg", "st", "ol", "of"] + ["ld" + k for k in LOADS] + ["ar%d" % t for t in range(4)]
BIG = 131072.0
TOP = 2097152
NACT = 6
MID = 12
SPLIT = (64, 64, 32, 48)


def rank_program(g, core, T, topo):
    rank = T.rank_of(core)
    if rank is None:
        return
    eng = {"v": g.vector, "a": g.scalar, "p": g.tensor, "g": g, "s": g.sync}
    sem = {"v": "sv", "a": "sa", "p": "sp", "g": "sg"}
    IDX, lastw, lastr, bank = {}, {}, {}, {}
    for k, s in list(PS.items()) + [(k, s) for k, (s, d) in SHAPES.items()]:
        n = int(np.prod(s))
        IDX[k] = np.arange(n).reshape(s)
        lastw[k] = np.full(n, -1)
        lastr[k] = {}
    ops = []
    count, clock = {}, {q: {} for q in eng}

    def S(a, b, st=None):
        return slice(a, b, st)
    ALL = S(None, None)

    def v(name, *idx):
        if name in SUB:
            name, o, n = SUB[name]
            a, b, st = idx[0].indices(n)
            idx = (S(o + a, o + b, st),)
        return {"n": name, "ap": T[name][(ALL,) + idx], "c": IDX[name][idx].ravel(), "off": None}

    def ind(win, off):
        return {"n": win["n"], "ap": win["ap"].indirect(off["ap"]), "c": win["c"], "off": off}

    def hazards(q, w, r):
        need = set()
        for x in list(r) + list(w):
            if not (q == "p" and x["n"] in PS):
                need.update(np.unique(lastw[x["n"]][x["c"]]).tolist())
        for x in w:
            for q2, a in lastr[x["n"]].items():
                need.add(int(a[x["c"]].max()))
        for x in list(w) + list(r):
            if x["n"] in PS:
                for b in np.unique(x["c"] // 512).tolist():
                    need.update(o for q2, o in bank.get((x["n"], b), {}).items() if q2 != q)
        need.discard(-1)
        return need

    def wait(q, need):
        ck, best = clock[q], {}
        for o in need:
            q2, n, c2 = ops[o]
            if ck.get(q2, 0) < n and (q2 not in best or ops[best[q2]][1] < n):
                best[q2] = o
        for q2 in sorted(best, key=lambda z: -best[z]):
            q2, n, c2 = ops[best[q2]]
            if ck.get(q2, 0) >= n:
                continue
            eng[q].wait_ge(T.sem[sem.get(q2, q2)], n)
            for k, x in c2.items():
                ck[k] = max(ck.get(k, 0), x)
            ck[q2] = n

    def note(q, tag, inc, w, r):
        count[tag] = count.get(tag, 0) + inc
        ops.append((tag, count[tag], dict(clock[q]) if q else {}))
        o = len(ops) - 1
        for x in w:
            lastw[x["n"]][x["c"]] = o
        for x in r:
            lastr[x["n"]].setdefault(tag, np.full(lastw[x["n"]].size, -1))[x["c"]] = o
        for x in list(w) + list(r):
            if x["n"] in PS:
                for b in np.unique(x["c"] // 512).tolist():
                    bank.setdefault((x["n"], b), {})[tag] = o
        return o

    def do(q, fn, w, r):
        r = r + [x["off"] for x in w + r if x["off"] is not None]
        wait(q, hazards(q, w, r))
        fn().then_inc(T.sem[sem[q]], 1)
        note(q, q, 1, w, r)

    def dma(q, tag, out, in_):
        w, r = ([out] if "n" in out else []), ([in_] if "n" in in_ else [])
        wait(q, hazards(q, w, r))
        eng[q].dma_start(out["ap"], in_["ap"]).then_inc(T.sem[tag], 16)
        return note(q, tag, 16, w, r)

    def col(s):
        return [s] if isinstance(s, dict) else []

    def num(s):
        return s["ap"] if isinstance(s, dict) else s

    def ts(out, a, s1, op0, s2=None, op1=None):
        if op1 is None:
            do("v", lambda: g.vector.tensor_scalar(out["ap"], a["ap"], num(s1), None, op0), [out], [a] + col(s1))
        else:
            do("v", lambda: g.vector.tensor_scalar(out["ap"], a["ap"], num(s1), num(s2), op0, op1), [out], [a] + col(s1) + col(s2))

    def tt(out, a, b, op):
        do("v", lambda: g.vector.tensor_tensor(out["ap"], a["ap"], b["ap"], op), [out], [a, b])

    def cp(out, a):
        do("v", lambda: g.vector.tensor_copy(out["ap"], a["ap"]), [out], [a])

    def fill(out, x):
        do("v", lambda: g.vector.memset(out["ap"], x), [out], [])

    def act(out, a, f=F.Identity, bias=0.0, scale=1.0):
        do("a", lambda: g.scalar.activation(out["ap"], a["ap"], f, bias=num(bias), scale=num(scale)), [out], [a] + col(bias) + col(scale))

    def mm(out, l, r, start, stop):
        do("p", lambda: g.tensor.matmul(out["ap"], l["ap"], r["ap"], start, stop), [out], [l, r])

    def iota(out, pat, base=0, cmul=0, small=True):
        if small:
            do("g", lambda: g.iota(out["ap"], pat, base, cmul, allow_small_or_imprecise_dtypes=True), [out], [])
        else:
            do("g", lambda: g.iota(out["ap"], pat, base, cmul), [out], [])

    def sel(out, a, pat, op, base, cmul):
        do("g", lambda: g.affine_select(out["ap"], a["ap"], pat, op, 0.0, base, cmul), [out], [a])

    for q, k, name in (("s", "wk", "wks"), ("a", "fm", "fmi"), ("s", "lm", "lmi"), ("a", "tl", "tli"), ("s", "mo", "MO"),
                       ("a", "sn", "sni"), ("s", "fr", "frs")):
        dma(q, "ld" + k, v(name, ALL), {"ap": T[k][:]})
    fill(v("ones", ALL), 1.0)
    sel(v("bg0", ALL), v("ones", ALL), [[-16, 8], [0, 16]], O.is_ge, 0, 1)
    sel(v("BG", ALL), v("bg0", ALL), [[16, 8], [0, 16]], O.is_ge, 15, -1)
    iota(v("pi", S(0, 1)), [[0, 1]], 0, 1, small=False)
    iota(v("nd", ALL), [[1, 16], [0, 16]])
    iota(v("ci16", ALL), [[1, 16]])
    iota(v("nm", ALL), [[0, 16], [1, 16]])
    sel(v("ID", ALL), v("ones", ALL), [[-1, 128]], O.is_equal, 0, 1)
    iota(v("jt", ALL), [[-1024, 16], [0, 16]])
    iota(v("zi", ALL), [[1, 16], [0, 4]])
    iota(v("ct16", ALL), [[16, 16]])
    iota(v("cn16", ALL), [[1024, 4], [16, 4]])
    iota(v("rt", ALL, ALL), [[256, 4], [0, 16]], 2048)
    sel(v("TSs", ALL), v("BG", ALL), [[1, 128]], O.is_gt, 0, -1)
    iota(v("itab", ALL), [[0, 4], [256, 16], [0, 64]])
    fill(v("LU", ALL, ALL), 0.0)
    fill(v("LV", ALL, ALL), 0.0)
    fill(v("EX", ALL, ALL), 0.0)
    cp(v("wkf", ALL), v("wks", ALL))
    ts(v("nwk", ALL), v("wkf", ALL), -1.0, O.mult)
    mp = [v("mp0", ALL), v("mp1", ALL)]
    act(mp[0], v("fmi", ALL), bias=255.0, scale=-1.0)
    for x in range(16):
        ts(v("LU", x, S(x, None, 16)), v("BG", S(x, None, 16)), v("nwk", S(0, 1)), O.mult)
        act(v("LV", x, S(x, None, 16)), v("BG", S(x, None, 16)), scale=v("nwk", S(1, 2)))
    ts(v("WU", ALL), v("BG", ALL), v("wkf", S(0, 1)), O.mult)
    ts(v("WV", ALL), v("BG", ALL), v("wkf", S(1, 2)), O.mult)
    fill(v("c255", ALL), 255.0)
    act(v("LM", S(16, 1040)), v("lmi", ALL), bias=255.0, scale=-1.0)
    ts(v("pm", S(0, 1)), v("pi", S(0, 1)), 15, O.bitwise_and)
    cp(v("pmf", S(0, 1)), v("pm", S(0, 1)))
    pmf = v("pmf", S(0, 1))
    ts(v("kr", ALL), v("nd", ALL), pmf, O.is_equal, v("wkf", S(2, 3)), O.mult)
    mm(v("PK", S(0, 256)), v("BG", ALL), v("kr", ALL), True, True)
    cp(v("kpat", ALL), v("PK", S(0, 256)))
    ts(v("repa", ALL), v("ci16", ALL), 0.0, O.mult, pmf, O.add)
    cp(v("repb", ALL), v("ci16", ALL))

    def late_constants():
        for x in range(16):
            act(v("EX", x, S(x, None, 16)), v("BG", S(x, None, 16)), scale=-BIG)
        ts(v("nI", ALL), v("ID", ALL), -1.0, O.mult)

    def later_constants():
        cp(v("IDf", ALL), v("ID", ALL))
        ts(v("nIf", ALL), v("ID", ALL), -1.0, O.mult)
        cp(v("BGf", ALL), v("BG", ALL))
        tt(v("TSf", ALL), v("BGf", ALL), v("IDf", ALL), O.subtract)
        ts(v("MD", ALL), v("nm", ALL), pmf, O.is_equal)
        tt(v("TSf", ALL), v("TSf", ALL), v("TSs", ALL), O.subtract)
        ts(v("zc", ALL), v("zi", ALL), 8192.0, O.mult, 15 * BIG + 2048, O.add)
        ts(v("eq", ALL), v("nm", ALL), 0.0, O.mult, pmf, O.is_equal)
        ts(v("lane", ALL), v("ct16", ALL), pmf, O.add)
        for r in range(2):
            ts(v("sd", r, ALL), v("lane", ALL), 1024.0, O.add)
        ts(v("dl", ALL), v("lane", ALL), 1040.0, O.add)
        ts(v("ds", ALL), v("lane", ALL), 6144.0, O.add)
        ts(v("ln8", ALL), v("lane", ALL), 8192.0, O.add)
        ts(v("nt", ALL), v("cn16", ALL), pmf, O.add)
        fill(v("cbig", ALL), BIG)
        fill(v("E", 0, S(0, 16)), 0.0)
        ts(v("TS", ALL), v("ID", ALL), -2048.0, O.mult)
        tt(v("TS", ALL), v("TS", ALL), v("TSs", ALL), O.add)

    far = [d for d in T.cores if d != core and topo.chip(d) != topo.chip(core)]
    near = [d for d in T.cores if d != core and topo.chip(d) == topo.chip(core)]
    lines, used = {}, set()
    for i, d in enumerate(far):
        e = topo.engines(core, d)
        lines[d] = e[i * 4:i * 4 + 4]
        used.update(e)
    for i, d in enumerate(near):
        lines[d] = [x for x in topo.engines(core, d) if x not in used][i * 8:i * 8 + 8]
    assert sum(len(x) for x in lines.values()) == 16
    for t in range(4):
        a, b = t * 160, t * 160 + rank * 40
        note(None, "ar%d" % t, 16, [v("rx", S(a, b)), v("rx", S(b + 40, a + 160))], [])

    def send(t):
        r = [v("se", S(T.rank_of(d) * 256, T.rank_of(d) * 256 + 40)) for d in far + near]
        wait("g", hazards("g", [], r))
        tr = []
        for d in far + near:
            rid, pid = topo.addr(d)[:2]
            a, b = T.rank_of(d) * 256, t * 160 + rank * 40
            tr.append(RemoteDMATransfer(dst_ids=[DstId(rid=rid, pnc=pid)], dma_engine_mask=sum(1 << e for e in lines[d]),
                                        remote_sem=T.sem["ar%d" % t], src=T.se[:, a:a + 40], dst=T.rx[:, b:b + 40]))
        g.remote_dma_fused(tr, local_sem=T.sem.st)
        note("g", "st", 16, [], r)

    def front_sums(m):
        for k, (L, W) in enumerate((("LU", "WU"), ("LV", "WV"))):
            o = v("PU0", S(16 * k, 16 * k + 16))
            mm(o, v(W, ALL), v("c255", S(0, 16)), True, False)
            for x in range(16):
                mm(o, v(L, x, ALL), v(m["n"], S(x, None, 16)), False, x == 15)

    def places1():
        cp(v("uvi", ALL), v("PU0", S(0, 32)))
        ts(v("uvm", ALL), v("uvi", ALL), 4095, O.bitwise_and)
        cp(v("uvf", ALL), v("uvm", S(0, 16)))
        tt(v("uvs", ALL), v("uvm", S(0, 16)), v("uvm", S(16, 32)), O.mult)
        ts(v("Aw", ALL), v("uvs", ALL), 5, O.arith_shift_right, 4095, O.bitwise_and)
        tt(v("kt", ALL), ind(v("uvf", ALL), v("repa", ALL)), v("kpat", ALL), O.mult)
        cp(v("Awf", ALL), v("Aw", ALL))

    def places2():
        tt(v("cc", ALL), ind(v("Awf", ALL), v("repa", ALL)), v("kt", ALL), O.add)
        ts(v("cm", ALL), v("cc", ALL), 1023, O.bitwise_and)
        cp(v("co", ALL), v("cm", ALL))

    def weave(a, b):
        for z in range(max(len(a), len(b))):
            for y in (a, b):
                if z < len(y):
                    y[z]()

    LMt, TLt, SNt = v("LM", S(16, 1040)), v("TL", S(16, 1040)), v("SN", S(2048, 6144))
    front_sums(mp[0])
    places1()
    places2()
    late_constants()
    cp(TLt, v("tli", ALL))

    for t in range(4):
        m, n = mp[t % 2], mp[(t + 1) % 2]
        A = list(range(16 - NACT, 16))

        def look(j):
            return ind(LMt, v("co", S(16 * j, 16 * j + 16)))

        def own(j):
            tt(v("V", S(256 * j, 256 * j + 256)), look(j), m, O.is_lt)

        def diff(k):
            gb_ = v(("ga", "gb")[(k // 2) % 2], S(256 * (k % 2), 256 * (k % 2) + 256))
            act(gb_, look(A[k]), F.Copy)
            o = v("PU%d" % ((k + 1) % 2), S(0, 256))
            mm(o, v("ID", ALL), m, True, False)
            mm(o, v("nI", ALL), gb_, False, True)

        def excess(k):
            act(v("V", S(256 * A[k], 256 * A[k] + 256)), v("PU%d" % ((k + 1) % 2), S(0, 256)), F.Relu)

        def tally(a, b, last=False):
            for x in range(16):
                mm(v("PK", S(16 * a, 16 * b)), v("EX", x, ALL), v("V", S(256 * a + x, 256 * b, 16)), False, last and x == 15)

        mm(v("PK", S(0, 256)), v("ID", ALL), v("jt", ALL), True, False)
        diff(0)
        diff(1)
        for j in range(16 - NACT):
            own(j)
        for k in range(2, NACT):
            excess(k - 2)
            diff(k)
            if k == 2:
                tally(0, 4)
            if k == 4:
                tally(4, 8)
        for k in range(NACT - 2, NACT):
            excess(k)
        if t == 0:
            later_constants()
        else:
            cp(ind(v("TL", ALL), v("oL16", ALL)), v("wt", ALL))
        if t < 3:
            a = 160 if t else 0
            act(v("ct", S(a, 256)), v("TL", S(16 + a, 272)), F.Copy)
        tally(8, MID)
        tally(MID, 16, True)
        tt(v("ka", ALL), v("cm", ALL), v("PK", S(0, 256)), O.subtract)
        tt(v("kc", S(0, 128)), v("ka", S(0, 128)), v("ka", S(128, 256)), O.min)
        tt(v("ka", S(0, 64)), v("kc", S(0, 64)), v("kc", S(64, 128)), O.min)
        tt(v("kc", S(0, 32)), v("ka", S(0, 32)), v("ka", S(32, 64)), O.min)
        tt(v("k1", ALL), v("kc", S(0, 16)), v("kc", S(16, 32)), O.min)
        ts(v("gi", ALL), v("k1", ALL), 1023, O.bitwise_and)
        cp(v("g16", ALL), v("gi", ALL))
        cp(v("tg", S(0, 64)), ind(TLt, v("g16", S(0, 4))))
        cp(v("tg", S(64, 256)), ind(TLt, v("g16", S(4, 16))))
        tt(v("ql", ALL), ind(LMt, v("g16", ALL)), m, O.subtract)

        def pick(k):
            act(v("Y", S(1024 * k, 1024 * k + 1024)), ind(v("MO", ALL), v("tg", S(64 * k, 64 * k + 64))), F.Copy)

        def minuend(k):
            for i in range(16):
                mm(v("PX%d" % (k % 2), S(64 * i, 64 * i + 64)), v("nI", ALL), v("ql", S(64 * k, 64 * k + 64)), i % 8 == 0, False)

        def products(k):
            for i in range(16):
                mm(v("PX%d" % (k % 2), S(64 * i, 64 * i + 64)), v("nI", ALL), v("Y", S(1024 * k + i, 1024 * k + 1024, 16)), False, i % 8 == 7)

        def clip(k):
            act(v("P", S(1024 * k, 1024 * k + 1024)), v("PX%d" % (k % 2), ALL), F.Relu, bias=255.0)

        def hsum(k):
            for z, (L, W) in enumerate((("LU", "WU"), ("LV", "WV"))):
                o = v("PU%d" % (k % 2), S(64 * z, 64 * z + 64))
                mm(o, v(W, ALL), v("c255", ALL), True, False)
                for x in range(16):
                    mm(o, v(L, x, ALL), v("P", S(1024 * k + x, 1024 * k + 1024, 16)), False, x == 15)

        def hash_(k):
            K, b = S(64 * k, 64 * k + 64), k % 2
            d, e = S(64 * b, 64 * b + 64), 128 * b
            return [lambda: cp(v("hi", S(e, e + 128)), v("PU%d" % b, S(0, 128))),
                    lambda: ts(v("hm", S(e, e + 128)), v("hi", S(e, e + 128)), 4095, O.bitwise_and),
                    lambda: tt(v("hs", d), v("hm", S(e, e + 64)), v("hm", S(e + 64, e + 128)), O.mult),
                    lambda: ts(v("ha", d), v("hs", d), 5, O.arith_shift_right, 4095, O.bitwise_and),
                    lambda: tt(v("hb", d), v("ha", d), v("hm", S(e, e + 64)), O.add),
                    lambda: ts(v("hc", K), v("hb", d), 4095, O.bitwise_and),
                    lambda: cp(v("h16", K), v("hc", K))]

        def seen(k):
            n1 = SPLIT[k]
            R = S(1024 * k, 1024 * k + 16 * n1)
            tt(v("M", R), ind(SNt, v("h16", S(64 * k, 64 * k + n1))), v("P", R), O.not_equal)

        def rows(k):
            K = S(64 * k, 64 * k + 64)
            return [lambda: tt(v("zk", K), v("hc", K), v("zc", ALL), O.add)]

        def seen2(k):
            n1 = SPLIT[k]
            R, o = S(1024 * k + 16 * n1, 1024 * k + 1024), v("PX%d" % (k % 2), S(0, 1024 - 16 * n1))
            act(v("Y", R), ind(SNt, v("h16", S(64 * k + n1, 64 * k + 64))), F.Copy)
            mm(o, v("ID", ALL), v("Y", R), True, False)
            mm(o, v("nI", ALL), v("P", R), False, True)
            act(v("M", R), o, F.Abs)

        def unequal(k):
            o = v("PK", S(64 * k, 64 * k + 64))
            mm(o, v("BG", ALL), v("cbig", ALL), True, False)
            for x in range(16):
                mm(o, v("EX", x, ALL), v("M", S(1024 * k + x, 1024 * k + 1024, 16)), False, x == 15)

        def least(k):
            a = 64 * k
            return [lambda: tt(v("kb", S(a, a + 64)), v("PK", S(a, a + 64)), v("zk", S(a, a + 64)), O.max),
                    lambda: tt(v("kd", S(a, a + 32)), v("kb", S(a, a + 32)), v("kb", S(a + 32, a + 64)), O.min),
                    lambda: tt(v("kb", S(a, a + 16)), v("kd", S(a, a + 16)), v("kd", S(a + 16, a + 32)), O.min),
                    lambda: tt(v("kd", S(a, a + 8)), v("kb", S(a, a + 8)), v("kb", S(a + 8, a + 16)), O.min),
                    lambda: tt(v("kz", S(4 * k, 4 * k + 4)), v("kd", S(a, a + 4)), v("kd", S(a + 4, a + 8)), O.min)]

        pick(0)
        minuend(0)
        minuend(1)
        products(0)
        pick(1)
        products(1)
        clip(0)
        pick(2)
        if t < 3:
            tt(v("yb", ALL), ind(v("Awf", ALL), v("repb", ALL)), v("MD", ALL), O.mult)
        if 0 < t < 3:
            ts(v("tla", ALL), v("xi", ALL), 12, O.arith_shift_right, 4095, O.bitwise_and)
            ts(v("cia", ALL), v("xi", ALL), 8, O.arith_shift_right, 15, O.bitwise_and)
            tt(v("tmi", ALL), v("TL", S(16, 176)), v("inv", ALL), O.mult)
            ts(v("eq", S(0, 160)), v("cia", ALL), pmf, O.is_equal)
            tt(v("ct", S(0, 160)), v("tla", ALL), v("tmi", ALL), O.add)
        side = [lambda: ts(v("nfb", ALL), v("k1", ALL), 16384.0, O.is_ge, float(TOP), O.mult),
                lambda: ts(v("nk0", ALL), v("k1", ALL), 16384.0, O.is_lt, 65536.0, O.mult),
                lambda: fill(v("se", S(0, 40)), -0.25),
                lambda: tt(v("nk1", ALL), v("cm", S(0, 16)), v("nk0", ALL), O.add),
                lambda: fill(v("se", S(256, 296)), -0.25),
                lambda: ts(v("nk0", ALL), v("nk1", ALL), 16.0, O.add),
                lambda: fill(v("se", S(512, 552)), -0.25),
                lambda: tt(v("nk", ALL), v("nk0", ALL), v("ln8", ALL), O.min),
                lambda: fill(v("se", S(768, 808)), -0.25)]
        hsum(0)
        clip(1)
        if t > 0:
            cp(ind(v("SN", ALL), v("oS16", ALL)), v("pc", ALL))
        else:
            ts(SNt, v("sni", ALL), -1.0, O.mult, 255.0, O.add)
        weave(hash_(0), [])
        minuend(2)
        products(2)
        hsum(1)
        pick(3)
        seen(0)
        clip(2)
        weave(rows(0) + hash_(1), side)
        minuend(3)
        products(3)
        unequal(0)
        hsum(2)
        seen(1)
        clip(3)
        weave(rows(1) + least(0), hash_(2))
        unequal(1)
        hsum(3)
        seen2(2)
        seen(2)
        act(v("t4", ALL), ind(TLt, v("g16", ALL)), scale=4096.0)
        weave(rows(2) + least(1), hash_(3))
        unequal(2)
        seen2(3)
        seen(3)
        weave(rows(3), [])
        weave(least(2), [])
        if t == 0:
            act(v("frs", ALL), v("frs", ALL), bias=255.0, scale=-1.0)
        act(v(n["n"], S(160, 256)), v("frs", S(t * 256 + 160, t * 256 + 256)), F.Copy)
        unequal(3)
        weave(least(3), [])
        tt(v("k3", ALL), v("kz", ALL), v("nfb", ALL), O.max)
        ts(v("rr", ALL), v("k3", ALL), TOP + 3, O.bitwise_and)
        ts(v("n0", ALL), v("k3", ALL), 7, O.arith_shift_right, 960, O.bitwise_and)
        for r in range(4):
            ts(v("D4", r, ALL), v("rr", ALL), float(r), O.is_equal)

        def pr(r0, r1, c0):
            return v("PM", S(r0, r1), S(c0, 16))
        mm(pr(0, 4, 0), v("TS", ALL), v("D4", ALL, ALL), True, False)
        mm(pr(0, 4, 0), v("ID", ALL), v("rt", ALL, ALL), False, False)
        for s in range(1, 16):
            mm(pr(0, 4, s), v("BG", ALL), v("D4", ALL, S(0, 16 - s)), False, s == 15)
        if t < 3:
            mm(v("PX0", S(0, 256)), v("BGf", ALL), v("yb", ALL), True, False)
            mm(v("PX0", S(0, 256)), v("nIf", ALL), v("ct", ALL), False, True)
        tt(v("n1", ALL), v("n0", ALL), v("nt", ALL), O.add)
        cp(v("n16", ALL), v("n1", ALL))
        act(v("pc", ALL), ind(v("P", ALL), v("n16", ALL)), F.Copy)
        tt(v("t1", ALL), ind(v("itab", ALL), v("n16", ALL)), v("t4", ALL), O.add)
        tt(v("o1", ALL, ALL), pr(0, 2, 0), v("sd", ALL, ALL), O.min)
        tt(v("o2", ALL, ALL), pr(2, 4, 0), v("o1", ALL, ALL), O.min)
        tt(v("o3", ALL), v("o2", 0, ALL), v("o2", 1, ALL), O.min)
        cp(v("s16", ALL), v("o3", ALL))
        tt(ind(v("se", ALL), v("s16", ALL)), v("t1", ALL), v("pc", ALL), O.add)
        send(t)
        q = S(t * 160, t * 160 + 160)
        act(v("rx", S(t * 160 + rank * 40, t * 160 + rank * 40 + 40)), v("se", S(rank * 256, rank * 256 + 40)), F.Copy)
        ts(v("hk", ALL), v("k3", ALL), TOP + 8191, O.bitwise_and)
        tt(v("key", ALL), v("hk", ALL), v("nk", ALL), O.min)
        tt(v("ya", ALL), ind(v("key", ALL), v("repb", ALL)), v("MD", ALL), O.mult)
        mm(v("PK", S(0, 256)), v("BGf", ALL), v("ya", ALL), True, True)
        mm(v("PX1", S(0, 256)), v("TSf", ALL), v("ya", ALL), True, True)
        cp(v("kw", ALL), v("PK", S(0, 256)))
        act(v("kdf", ALL), v("PX1", S(0, 256)), F.Copy)
        act(v("inv", ALL), v("rx", q), F.Relu, scale=-4.0)
        for c in range(15):
            z = 16 if c == 0 else 0
            ts(v("E", c, S(z, z + 240 - 16 * c)), v("kw", S(16 * c + 16, 256)), v("key", S(c, c + 1)), O.is_equal)
            mm(v("PK", S(16 * c + 16 - z, 256)), v("BG", ALL), v("E", c, S(0, z + 240 - 16 * c)), c == 0, False)
            if c == 7:
                tt(v("E", 15, ALL), ind(v("key", ALL), v("repb", ALL)), v("kdf", ALL), O.is_equal)
        mm(v("PK", S(0, 256)), v("BG", ALL), v("E", 15, ALL), False, True)
        act(v("dub", ALL), v("PK", S(0, 256)), F.Copy)
        cp(v("xi", ALL), v("rx", q))
        tt(v("ri", ALL), v("frs", S(t * 256, t * 256 + 160)), v("inv", ALL), O.mult)
        ts(v("pa", ALL), v("xi", ALL), 255, O.bitwise_and)
        tt(v(n["n"], S(0, 160)), v("pa", ALL), v("ri", ALL), O.add)
        if t < 3:
            front_sums(n)
        else:
            act(v("ga", S(0, 256)), n, bias=255.0, scale=-1.0)
            o2 = dma("s", "of", {"ap": T.yf[:]}, v("ga", S(0, 256)))
        for x in range(16):
            mm(v("PM", 20, ALL), v("EX", x, ALL), v("dub", S(x, None, 16)), x == 0, x == 15)
        if t < 3:
            tt(v("wd", ALL), v("PX0", S(0, 256)), v("eq", ALL), O.mult)
            mm(v("PX0", S(256, 512)), v("IDf", ALL), v("ct", ALL), True, False)
            mm(v("PX0", S(256, 512)), v("IDf", ALL), v("wd", ALL), False, True)
            act(v("wt", ALL), v("PX0", S(256, 512)), F.Copy)
            places1()
        ts(v("los", ALL), v("PM", 20, ALL), -1.0, O.is_le, 65536.0, O.mult)
        tt(v("kl", ALL), v("key", ALL), v("los", ALL), O.add)
        tt(v("oL", ALL), v("kl", ALL), v("dl", ALL), O.min)
        cp(v("oL16", ALL), v("oL", ALL))
        cp(ind(v("LM", ALL), v("oL16", ALL)), m)
        if t < 3:
            places2()
            tt(v("oS", ALL), v("kl", ALL), v("ds", ALL), O.min)
            cp(v("oS16", ALL), v("oS", ALL))
        else:
            act(v("Y", S(0, 1024)), LMt, bias=255.0, scale=-1.0)
            o1 = dma("s", "ol", {"ap": T.yl[:]}, v("Y", S(0, 1024)))
            wait("s", [o1])
            wait("s", [o2])
    for tag in ("st", "v", "a", "p", "g"):
        wait("g", [[i for i, o in enumerate(ops) if o[0] == tag][-1]])
